import numpy as np, ml_dtypes
CORES = [36,164,52,180,100,228,116,244]
N = 8
BF = ml_dtypes.bfloat16
def gentries(a):
    return np.ascontiguousarray(a.reshape(8, 16, -1).transpose(0, 2, 1)).reshape(8, -1)
def gtable(e):
    e = np.asarray(e); return np.ascontiguousarray(e.reshape(8, -1, 16).transpose(0, 2, 1)).reshape(128, -1).astype(np.int32)
C, K0, NQ, T, L, DS, SB = 3072, 128, 128, 2, 5, 4, 14
KM = K0 + T * NQ
def machine(rng, k, p, q):
    cl = rng.permutation(np.concatenate([np.arange(k), rng.integers(0, k, C - k)]))
    o = np.argsort(cl, kind="stable"); size = np.bincount(cl, minlength=k); first = np.add.accumulate(size) - size
    x = rng.integers(0, k, (16, k))[:, cl]; nx = o[first[x] + rng.integers(0, size[x])]
    out = rng.integers(0, 16, (16, k))[:, cl]
    out = np.where(rng.random((16, C)) < p, rng.integers(0, 16, (16, C)), out)
    nx = np.where(rng.random((16, C)) < q, rng.integers(0, C, (16, C)), nx)
    return nx, out, cl
def machines(rng):
    nx = np.empty((N, 8, 16, C), np.int64); out = np.empty((N, 8, 16, C), np.int64)
    for r in range(N):
        for g in range(8):
            p = float(rng.choice(np.array([0.004, 0.01, 0.03])))
            nx[r, g], out[r, g], cl = machine(rng, int(rng.choice(np.array([30, 80, 200, 500]))), p, 0.3 * p)
    return nx, out
def others(rng):
    return (rng.integers(0, C, (N, 8, K0)), rng.integers(0, 2 ** SB, (N, 8, T, NQ)), rng.integers(0, 16, (N, 8, T, NQ)),
            rng.integers(0, 16, (N, 8, 16, L)), rng.integers(0, 16, (N, 8, T, 16, L)))
def fresh(rng, ex):
    b = C // (T + 1); c = np.arange(C)
    nx = rng.integers(0, C, (16, C)); out = rng.integers(0, 16, (16, C)); nx[15] = c
    for d in range(3): out[d] = (c >> (4 * d)) & 15
    for t in range(T): nx[3 + t] = (t + 1) * b + rng.integers(0, b, C)
    ex[13:] = 15; ex[13:, L - 1] = np.arange(3)
    return nx, out, rng.integers(0, b, K0), np.repeat(3 + np.arange(T), NQ).reshape(T, NQ)
def pack(nx, out, bk, qs, qc, ex, zs):
    return {"mt": np.ascontiguousarray(np.roll((16 * nx + out).reshape(N, 128, C), DS, axis=0)).astype(np.int32),
            "bk": np.stack([gtable(a) for a in bk]), "qs": np.stack([gtable(a.reshape(8, -1)) for a in qs]), "qc": np.stack([gtable(a.reshape(8, -1)) for a in qc]),
            "ex": np.ascontiguousarray(ex.reshape(N, 128, L)).astype(np.int32), "zs": np.ascontiguousarray(zs.transpose(0, 1, 3, 2, 4)).reshape(N, 128, T * L).astype(np.int32)}
def setup_inputs(rng):
    nx, out = machines(rng)
    return pack(nx, out, *others(rng))
def setup_inputs_grow(rng):
    nx, out = machines(rng); bk, qs, qc, ex, zs = others(rng); c = np.arange(C); h = C // 2
    for r in range(N):
        o = rng.permutation(8)
        for g in o[:3]: nx[r, g], out[r, g], bk[r, g], qc[r, g] = fresh(rng, ex[r, g])
        g = o[2]; nx[r, g, 4:3 + T] = np.where(c >= C // (T + 1), c, nx[r, g, 4:3 + T])
        qs[r, g, 1:, :8] = 2 ** SB - 1 - np.arange(8) * (2 ** SB // (K0 + NQ))
        for g in o[3:6]:
            k = int(rng.integers(20, 61)); nx[r, g], out[r, g], cl = machine(rng, k, 0.0, 0.0)
            one = np.unique(cl, return_index=True)[1]
            bk[r, g] = rng.permutation(np.concatenate([one, rng.integers(0, C, K0 - k)]))
        g = o[5]
        nx[r, g, 15] = c; out[r, g, 15] = np.where(c < h, 3, 9); nx[r, g, 14, :h] = rng.integers(h, C, h)
        one = np.unique(cl[:h], return_index=True)[1]
        bk[r, g] = rng.permutation(np.concatenate([one, rng.integers(0, h, K0 - len(one))]))
        qc[r, g, 0] = 14; ex[r, g] = rng.integers(0, 14, (16, L)); zs[r, g, 0, int(rng.integers(1, 16))] = 15
    return pack(nx, out, bk, qs, qc, ex, zs)
def setup_inputs_near(rng):
    nx = np.empty((N, 8, 16, C), np.int64); out = np.empty((N, 8, 16, C), np.int64); bk, qs, qc, ex, zs = others(rng)
    for r in range(N):
        for g in range(8):
            x, y, cl = machine(rng, 40, 0.0, 0.0); y = np.minimum(np.maximum(y, 1), 14); x[15] = np.arange(C)
            c = np.flatnonzero(rng.random(C) < 0.5); a = rng.integers(0, 16, len(c)); b = (a + rng.integers(1, 16, len(c))) & 15
            y[a, c] += 1
            if (r + g) & 1: y[b, c] -= 1
            nx[r, g] = x; out[r, g] = y; ex[r, g] = 15; ex[r, g, :, L - 1] = rng.permutation(16)
    return pack(nx, out, bk, qs, qc, ex, zs)
def setup_inputs_alike(rng):
    nx, out = machines(rng); bk, qs, qc, ex, zs = others(rng)
    bk[:, ::2] = np.take_along_axis(rng.integers(0, C, (N, 4, 6)), rng.integers(0, 6, (N, 4, K0)), 2)
    zs = np.take_along_axis(zs, rng.integers(0, 5, (N, 8, T, 16))[..., None], 3)
    ex[:, 1::4] = np.repeat(ex[:, 1::4, :4], 4, axis=2)
    qs[:, 3] = rng.integers(0, 2 ** SB, 4)[rng.integers(0, 4, (N, T, NQ))]; qc[:, 3] = rng.integers(0, 16, 2)[rng.integers(0, 2, (N, T, NQ))]
    for r in range(N):
        nx[r, 5], out[r, 5], bk[r, 5], qc[r, 5] = fresh(rng, ex[r, 5])
        qs[r, 5] = rng.integers(0, 2 ** SB, 3)[rng.integers(0, 3, (T, NQ))]
    c = np.arange(C)
    nx[:, 7] = np.where(rng.random((N, 16, C)) < 0.1, 0, rng.integers(0, C, (N, 16, C))); nx[:, 7, 15] = c
    out[:, 7] = np.where((c == 0) | (c >= C // 2), 0, rng.integers(1, 16, (N, 16, C)))
    out[1::2, 7] = 15 - out[1::2, 7]
    bk[:, 7] = rng.integers(1, C // 2, (N, K0)); qc[:, 7] = rng.integers(0, 15, (N, T, NQ))
    ex[:, 7] = 15; ex[:, 7, :, L - 1] = np.argsort(rng.random((N, 16)), axis=-1)
    for r in range(N):
        if r & 2:
            nx[r, 7, 14] = np.where(rng.random(C) < 0.5, bk[r, 7][rng.integers(0, K0, C)], rng.integers(1, C // 2, C))
            qc[r, 7, 0] = 14; zs[r, 7, :, :, :L - 1] = 15
    return pack(nx, out, bk, qs, qc, ex, zs)
def setup_inputs_ends(rng):
    nx, out = machines(rng); bk, qs, qc, ex, zs = others(rng); e = np.array([0, C - 1]); l = np.array([0, 15])
    nx = np.where(rng.random(nx.shape) < 0.2, e[rng.integers(0, 2, nx.shape)], nx)
    qs[:, ::2] = np.array([0, 2 ** SB - 1])[rng.integers(0, 2, (N, 4, T, NQ))]
    qs[:, 1::2, 0] = (rng.integers(0, K0, (N, 4, NQ)) * (2 ** SB // K0) - rng.integers(0, 2, (N, 4, NQ))) & (2 ** SB - 1)
    qc[:, 1] = l[rng.integers(0, 2, (N, T, NQ))]; bk[:, 2] = e[rng.integers(0, 2, (N, K0))]; bk[:, :, 0] = 0; bk[:, :, K0 - 1] = C - 1
    ex[:, 4] = l[rng.integers(0, 2, (N, 16, L))]; zs[:, 4] = l[rng.integers(0, 2, (N, T, 16, L))]; ex[:, 5] = 15; zs[:, 7] = 0
    return pack(nx, out, bk, qs, qc, ex, zs)
def setup_inputs_spread(rng):
    a = rng.choice(np.array([1, 3, 8]), (N, 8, 1, 1)); b = rng.choice(np.array([1, 2, 6]), (N, 8, 1, 1))
    nx = (C * rng.random((N, 8, 16, C)) ** a).astype(np.int64); out = (16 * rng.random((N, 8, 16, C)) ** b).astype(np.int64)
    bk = (C * rng.random((N, 8, K0)) ** a[..., 0]).astype(np.int64); qs = (2 ** SB * rng.random((N, 8, T, NQ)) ** b).astype(np.int64)
    qc = (16 * rng.random((N, 8, T, NQ)) ** 2).astype(np.int64)
    ex = (16 * rng.random((N, 8, 16, L)) ** 2).astype(np.int64); zs = (16 * rng.random((N, 8, T, 16, L)) ** 2).astype(np.int64)
    return pack(nx, out, bk, qs, qc, ex, zs)
def check_inputs(d):
    bad = []
    for k, hi in (("mt", 16 * C - 1), ("bk", C - 1), ("qs", 2 ** SB - 1), ("qc", 15), ("ex", 15), ("zs", 15)):
        if np.min(d[k]) < 0 or np.max(d[k]) > hi: bad.append("range of " + k)
    return bad
def walk(tb, q, w):
    r = np.arange(N)[:, None, None, None]; g = np.arange(8)[None, :, None, None]; s = q[:, :, None, :]
    for i in range(L):
        v = tb[r, g, w[:, :, :, i][..., None], s]; s = v >> 4
    return v & 15
def reference(mt, bk, qs, qc, ex, zs):
    tb = np.roll(mt.astype(np.int64), -DS, axis=0).reshape(N, 8, 16, C)
    s_ = np.stack([gentries(a) for a in qs]).astype(np.int64).reshape(N, 8, T, NQ); c_ = np.stack([gentries(a) for a in qc]).astype(np.int64).reshape(N, 8, T, NQ)
    E = ex.astype(np.int64).reshape(N, 8, 16, L); Z = zs.astype(np.int64).reshape(N, 8, 16, T, L)
    kn = np.zeros((N, 8, KM), np.int64); rec = np.zeros((N, 8, 16, KM), np.int64); cnt = np.full((N, 8, 1), K0, np.int64)
    kn[:, :, :K0] = np.stack([gentries(a) for a in bk]); rec[..., :K0] = walk(tb, kn[:, :, :K0], E)
    r3 = np.arange(N)[:, None, None]; g3 = np.arange(8)[None, :, None]; ms = []
    for t in range(T):
        b = np.take_along_axis(kn, (s_[:, :, t] * cnt) >> SB, 2)
        q = tb[r3, g3, c_[:, :, t], b] >> 4
        rq = walk(tb, q, E)
        eq = np.broadcast_to((np.arange(KM) < cnt)[:, :, None, :], (N, 8, NQ, KM))
        for e in range(16): eq = eq & (rq[:, :, e, :, None] == rec[:, :, e, None, :])
        hit = np.any(eq, axis=3); new = (~hit).astype(np.int64)
        m = np.where(hit, np.argmax(eq, axis=3), cnt + np.add.accumulate(new, axis=2) - new)
        i, j, n = np.nonzero(new)
        kn[i, j, m[i, j, n]] = q[i, j, n]; rec[i, j, :, m[i, j, n]] = rq[i, j, :, n]
        cnt = cnt + np.add.reduce(new, axis=2)[..., None]; ms.append(m)
        zt = Z[:, :, :, t]
        differ = walk(tb, q, zt) != walk(tb, np.take_along_axis(kn, m, 2), zt)
        best = np.argmax(np.add.reduce(differ.astype(np.int64), axis=3), axis=2)
        E[:, :, t] = zt[r3[..., 0], g3[..., 0], best]
        rec[:, :, t] = walk(tb, kn, E[:, :, t:t + 1])[:, :, 0]
    rec = np.where((np.arange(KM) < cnt)[:, :, None, :], rec, -1)
    return {"ym": np.concatenate(ms, axis=2).astype(np.float32), "yr": rec.reshape(N, 128, KM).astype(np.float32), "ye": E.reshape(N, 128, L).astype(np.float32)}

@@ -1,0 +1,458 @@
+from concourse.mybir import AluOpType, AxisListType, ActivationFunctionType
+
+AL = AluOpType
+AF = ActivationFunctionType
+C = 3072
+HALF = 1536.0
+CH = [0, 1024, 2048, 2816, 3072]
+STREAMS = ["b", "q", "r", "Eb", "Eq", "Yb", "Yq", "Zb", "Zq", "Er", "Zr"]
+CFG = {"split": {k: 1 if k in ("Yb", "Yq", "Zb", "Zq") else 2 for k in STREAMS}, "turn": []}
+ORDER = ("00020406080m0s0g0a1a16180c2q1c2e1s1e1g1o0e1k1q24302k2a2m0o0r101u1y0v222t0i0k2h34202x122z281w1m382c3i33373k3b3t4c4e3e0w4h3g1i"
+         "4k4m143m3o4p4r4v3q404y4i526a50574s6654596c446g9w80685a826e3c5e5g857e7g7j6m6i5k8646425q6o5c6k6t888b7k6q6u5t0y488o9a5i5m7m8r8t"
+         "6y6w7o727q708c7t5o5v5x748e768u7u7a7d79a15y61627w8g65a49zaiak8xa6aaama89daoasaqacag3vaea2au264a2uawb02pb2ayb44w7y8i8kb88m3x9f"
+         "ba9gbcbebgbi8zbubwbybkbnc0c29ibrc490c6bo9lc8cacgci92ceckdwcccmcocqcscucwdye4e0czd0d4d69me2dad3d9dcdedkdge7e8eadjdneceg9pfedo"
+         "drdsdufbekf8efen9qfcfyg0fmfqejetfgfofsfifk95eoewg2fwfueqev2ig49s9vg6gcga3zg8gef0gigkgogqggezb69698bsgsf2f4gmguf6h4h6h9hghahc"
+         "hehihkhmgwgyh0h2hohqhs")
+NB = 8
+F32, BF, F16, I32, U16 = "float32", "bfloat16", "float16", "int32", "uint16"
+SB = {"snd": (55, I32), "inp": (55, I32), "lu": (56, U16), "tb": (C, I32), "xi": (C, I32), "oi": (C, I32),
+      "ic": (256, F32), "cd": (128, F32), "jc": (12, F32), "ri": (4, I32), "pc": (16, F32),
+      "id16": (16, BF), "w2": (144, BF), "w1": (144, F16), "blk": (128, F32), "ind8": (128, F32), "indk": (8, BF),
+      "idf": (128, F32), "idb": (128, BF), "keep0": (128, BF), "keep1": (128, BF), "ee": (256, BF), "kv": (256, BF),
+      "rows": (384, F32), "zsrc": (1024, BF), "so": (12, U16), "so2": (2, U16), "st": (4, U16), "sm": (1152, BF),
+      "vo": (240, BF), "vo2": (80, BF), "elu": (6, U16), "qm": (256, BF), "kl": (16, U16), "sf": (8, F32),
+      "nxc": (512, I32), "nxq": (128, I32), "t16": (256, F16), "ql": (16, U16), "dup": (256, BF),
+      "rea": (264, BF), "ry": (264, BF), "zc": (648, BF), "zq": (128, BF), "rc": (512, BF), "rq": (128, BF), "rt": (136, BF),
+      "qh": (512, BF), "q2": (256, BF), "r2": (384, BF), "mn": (16, F32), "nh": (256, F32), "cum": (256, F32),
+      "tt": (256, F32), "ls": (512, F16), "yms": (256, F32), "ll": (32, U16), "df": (272, BF), "sc": (4, F32), "sd": (32, F32),
+      "ww": (288, BF), "fin": (29, F32), "finl": (29, F32), "rcl": (384, BF), "rcf": (384, F32)}
+for _k in range(6):
+    SB["pb%d" % _k] = (4096, BF)
+for _k in STREAMS:
+    SB["g" + _k] = (2048, F16)
+    SB["o" + _k] = (128, U16)
+    SB["u" + _k] = (128, F16)
+SCRATCH = {k: ("sbuf", [128, v[0]], v[1]) for k, v in SB.items()}
+SCRATCH["yd"] = ("dram", [128, 16], F32)
+SCRATCH["yl"] = ("dram", [128, 16], F32)
+for _k in range(NB):
+    SCRATCH["ps%d" % _k] = ("psum", [128, 512], F32)
+SEMAPHORES = ["cV", "cA", "cP", "cG", "ldin", "tb0", "tb1", "tb2", "tb3", "z1", "z3", "z5", "ymd", "oym", "oyr", "ofin",
+              "lsem", "ainp", "aym", "arc", "afin"]
+
+
+def make_ops(g, T, peer, cfg):
+    ops = []
+    rid, pid, mask, nen = peer
+    split, turn = cfg["split"], cfg["turn"]
+    V = g.vector
+    Q = {"A": g.scalar, "S": g.sync}
+    sets = [("Eb", "Eq", "Er"), ("Yb", "Yq"), ("Zb", "Zq", "Zr")]
+    need_t = [any(s in turn for s in w) for w in sets]
+    need_d = [any(s not in turn for s in w) for w in sets]
+
+    def op(name, eng, cost, r, w, fn, pw=None, pr=None, sem=None):
+        ops.append({"n": name, "e": eng, "c": cost, "r": r, "w": w, "f": fn, "pw": pw, "pr": pr, "sem": sem})
+
+    def lin(e, out, in_, scale=1.0, bias=0.0):
+        if e == "V":
+            return V.tensor_scalar(out, in_, scale, bias, AL.mult, AL.add)
+        return g.scalar.activation(out, in_, AF.Copy if isinstance(bias, float) else AF.Identity, bias=bias, scale=scale)
+
+    def col(j):
+        return T.pc[:, j:j + 1]
+
+    def pcr(j):
+        return ("pc", j, j + 1)
+
+    def ts(name, cost, r, w, out, in0, s1, s2, *o):
+        op(name, "V", cost, r, w, lambda e, ps: V.tensor_scalar(out, in0, s1, s2, *o))
+
+    def eq(buf, n, src, j, p=128):
+        ts(buf, ("c1", n), [(src, 0, n), pcr(j)], [(buf, 0, n)], T[buf][0:p, 0:n], T[src][0:p, 0:n], T.pc[0:p, j:j + 1], None, AL.is_equal)
+
+    def li(name, cost, r, w, out, in_, scale=1.0, bias=0.0, eng="VA"):
+        op(name, eng, cost, r, w, lambda e, ps: lin(e, out, in_, scale, bias))
+
+    def lp(name, tile, a, b, r, w, out, scale=1.0, bias=0.0, p=128):
+        op(name, "VA", ("c1", b - a), r, w, lambda e, ps: lin(e, out, ps[0:p, a:b], scale, bias), pr=tile)
+
+    def fill(name, buf, a, b, val, kind="ch"):
+        def f(e, ps):
+            if e == "V":
+                return V.memset(T[buf][:, a:b], val)
+            return lin(e, T[buf][:, a:b], T.zsrc[:, 0:b - a], 0.0, float(val))
+        op(name, "VA", (kind, b - a), [("zsrc", 0, 1024)], [(buf, a, b)], f)
+
+    def dma(name, q, t, r, w, pairs, sem):
+        op(name, q, ("dma", t), r, w, lambda e, ps: [Q[e].dma_start(o, i) for o, i in pairs], sem=(sem, 16 * len(pairs)))
+
+    def send(name, t0, t1, r, w, out, in_):
+        op("s" + name, "G", ("rem", t0), [r], [("x" + name, 0, 1)],
+           lambda e, ps: g.remote_dma(out, in_, T.sem["a" + name], T.sem.lsem, pid, rid, mask), sem=("lsem", nen))
+        op("a" + name, "X", ("arr", t1), [("x" + name, 0, 1)], [w], None, sem=("a" + name, nen))
+
+    def pe(name, n, r, seq):
+        def f(e, ps):
+            last = None
+            for out, l, rr, st, sp in seq(ps):
+                last = g.tensor.matmul(out, l, rr, st, sp)
+            return last
+        op("p" + name, "P", ("pe", n), r, [], f, pw=name)
+
+    def iota(buf, n, pat):
+        op("i" + buf, "G", ("io", n), [], [(buf, 0, n)], lambda e, ps: g.iota(T[buf][:, 0:n], pat, 0, 0, allow_small_or_imprecise_dtypes=True))
+
+    def scat(name, n, r, wbuf, a, b, offs, src):
+        op(name, "V", ("s", n), r, [(wbuf, a, b)], lambda e, ps: V.tensor_copy(T[wbuf][:, a:b].indirect(offs), src))
+
+    dma("ldin", "S", 2.2, [], [("snd", 0, 55)], [(T.snd[:, 0:8], T.bk[:]), (T.snd[:, 40:45], T.ex[:]), (T.snd[:, 45:55], T.zs[:]),
+                                                 (T.snd[:, 8:24], T.qs[:]), (T.snd[:, 24:40], T.qc[:])], "ldin")
+    for k in range(4):
+        a, b = CH[k], CH[k + 1]
+        dma("tb%d" % k, "A", 2.5 + 5.0 * b / C, [], [("tb", a, b)], [(T.tb[:, a:b], T.mt[:, a:b])], "tb%d" % k)
+    op("ri0", "G", ("io", 1), [], [("ri", 0, 1)], lambda e, ps: g.iota(T.ri[:, 0:1], [[0, 1]], 0, 1))
+    iota("ic", 256, [[1, 256]])
+    iota("jc", 12, [[0, 3], [0, 2], [2048, 2]])
+    iota("cd", 128, [[1, 8], [0, 16]])
+    INP = ("inp", 0, 55)
+    send("inp", 1.0, 4.0, ("snd", 0, 55), INP, T.inp[:], T.snd[:])
+
+    wid = [4096 if d else 2048 for d in need_d]
+    op("zsrc", "V", ("ch", 1024), [], [("zsrc", 0, 1024)], lambda e, ps: V.memset(T.zsrc[:], 0.0))
+    for k in range(wid[0] // 1024):
+        fill("zp0_%d" % k, "pb0", 1024 * k, 1024 * k + 1024, 0.0)
+    iota("pb2", wid[1], [[0, wid[1]]])
+    iota("pb4", wid[2], [[0, wid[2]]])
+    n = 0
+    for w in range(3):
+        if need_d[w]:
+            b = "pb%d" % (2 * w + 1)
+            dma("z" + b, "S", 5.0 + 4.0 * n, [("zsrc", 0, 1024), ("tb", 0, C)], [(b, 0, 4096)],
+                [(T[b][:, 1024 * j:1024 * j + 1024], T.zsrc[:]) for j in range(4)], "z%d" % (2 * w + 1))
+            n += 1
+        if need_t[w]:
+            fill("zsm%d" % w, "sm", 384 * w, 384 * w + 384, 0.0)
+
+    for j, (c, o) in enumerate(((15, AL.bitwise_and), (4, AL.arith_shift_right), (16, AL.bitwise_and))):
+        ts("ri%d" % (j + 1), ("c1", 1), [("ri", 0, 1)], [("ri", j + 1, j + 2)], T.ri[:, j + 1:j + 2], T.ri[:, 0:1], c, None, o)
+    li("pc0", ("c1", 4), [("ri", 0, 4)], [("pc", 0, 4)], T.pc[:, 0:4], T.ri[:])
+    for j, src, sc, bi in ((4, 0, 16.0, 15.0), (6, 2, 16.0, 15.0), (7, 3, 128.0, -2048.0), (8, 3, -128.0, 0.0), (9, 3, -64.0, 1024.0), (10, 3, 64.0, 0.0)):
+        li("pc%d" % j, ("c1", 1), [pcr(src)], [pcr(j)], col(j), col(src), sc, bi)
+    li("pc5", ("c1", 1), [pcr(0), pcr(1)], [pcr(5)], col(5), col(1), 128.0, col(0))
+    icr = ("ic", 0, 256)
+    eq("id16", 16, "ic", 1)
+    li("pc11", ("c1", 2), [("id16", 0, 16), pcr(0)], [("pc", 11, 13)], T.pc[:, 11:13], T.id16[:, 0:2], -1000.0, col(0))
+    eq("w2", 144, "ic", 6)
+    eq("w1", 144, "ic", 4, 8)
+    eq("blk", 128, "cd", 2)
+    eq("ind8", 128, "cd", 0, 8)
+    eq("idf", 128, "ic", 0)
+    eq("keep0", 128, "ic", 11)
+    eq("keep1", 128, "ic", 12)
+    ts("indk", ("c1", 8), [icr, pcr(2)], [("indk", 0, 8)], T.indk[:], T.ic[:, 0:8], col(2), 1024.0, AL.is_equal, AL.mult)
+    if turn:
+        eq("idb", 128, "ic", 0)
+        li("pc13", ("c1", 1), [pcr(1), pcr(2)], [pcr(13)], col(13), col(1), 8.0, col(2))
+        li("st", ("c1", 3), [icr, pcr(13)], [("st", 0, 4)], T.st[:, 0:3], T.ic[:, 0:3], 128.0, col(13))
+    for h in range(2):
+        li("ee%d" % h, ("c1", 128), [icr, pcr(9 + h)], [("ee", 128 * h, 128 * h + 128)], T.ee[:, 128 * h:128 * h + 128], T.ic[:, 0:128], 0.0, col(9 + h))
+        li("dfc%d" % h, ("c1", 1), [pcr(1)], [("df", 136 * h + 128, 136 * h + 129)], T.df[:, 136 * h + 128:136 * h + 129], col(1), -1.0 / 16, 1.0)
+    li("kv", ("c1", 256), [icr], [("kv", 0, 256)], T.kv[:], T.ic[:], 2.0 ** -14, 0.0)
+    for j, (sc, bi) in enumerate(((1.0, 512.0), (-1.0, -384.0), (0.0, 1.0))):
+        li("row%d" % j, ("c1", 128), [icr], [("rows", 128 * j, 128 * j + 128)], T.rows[0:8, 128 * j:128 * j + 128], T.ic[0:8, 0:128], sc, bi)
+    fill("frc", "rc", 128, 512, -1.0)
+    fill("fzc", "zc", 128, 512, -1.0)
+    fill("fnx", "nxc", 128, 256, 0, "c1")
+    li("soc", ("c1", 12), [("jc", 0, 12), pcr(5)], [("so", 0, 12)], T.so[:], T.jc[:], 1.0, col(5))
+    li("so2c", ("c1", 1), [pcr(5)], [("so2", 1, 2)], T.so2[:, 1:2], col(5), 1.0, 2048.0)
+
+    RND = -0.46875
+    for k in range(4):
+        a, b = CH[k], CH[k + 1]
+        li("x%d" % k, ("c1", b - a), [("tb", a, b)], [("xi", a, b)], T.xi[:, a:b], T.tb[:, a:b], 1.0 / 16, RND)
+        ts("o%d" % k, ("c1", b - a), [("tb", a, b)], [("oi", a, b)], T.oi[:, a:b], T.tb[:, a:b], 15, None, AL.bitwise_and)
+    XI, OI, TB = ("xi", 0, C), ("oi", 0, C), ("tb", 0, C)
+
+    LU, ID, SO, VO = ("lu", 0, 55), ("id16", 0, 16), ("so", 0, 12), ("vo", 0, 240)
+    li("lu", ("c1", 55), [INP], [LU], T.lu[:, 0:55], T.inp[:])
+    li("k0", ("c1", 8), [INP], [("kl", 0, 8)], T.kl[:, 0:8], T.inp[:, 8:16], 1.0 / 128, -0.5 + 1.0 / 256)
+    li("sf", ("c1", 8), [INP], [("sf", 0, 8)], T.sf[:], T.inp[:, 16:24], 2.0 ** -14, 0.0)
+    li("sod", ("c1", 3), [INP, pcr(0)], [SO], T.so[:, 0:12:4], T.inp[:, 40:55:5], 128.0, col(0))
+    li("vo", ("g", 240), [LU, ID], [VO], T.vo[:], T.id16[:].indirect(T.lu[:, 40:55]))
+    li("qm", ("g", 256), [LU, ID], [("qm", 0, 256)], T.qm[:], T.id16[:].indirect(T.lu[:, 24:40]))
+    for b, a, c in (("rea", 256, 40), ("ry", 256, 45), ("zc", 640, 50)):
+        li("let" + b, ("c1", 5), [INP], [(b, a, a + 5)], T[b][:, a:a + 5], T.inp[:, c:c + 5])
+
+    def onehots(tag, w, vo, vr, v0, so, s0, sr):
+        k = wid[w] // 2048
+        scat(tag + "a", 16 * k, [sr, vr], "pb%d" % (2 * w), 0, wid[w], so[:, s0:s0 + k], vo[:, v0 + 16:v0 + 16 + 16 * k])
+        if need_d[w]:
+            scat(tag + "b", 32, [SO, vr], "pb%d" % (2 * w + 1), 0, 4096, T.so[:, 2:4], vo[:, v0 + 48:v0 + 80])
+        if need_t[w]:
+            scat(tag + "c", 48, [("st", 0, 4), vr], "sm", 384 * w, 384 * w + 384, T.st[:, 0:3], vo[:, v0 + 32:v0 + 80])
+
+    for w in range(3):
+        onehots("sp%d" % w, w, T.vo, VO, 80 * w, T.so, 4 * w, SO)
+
+    def parts(s):
+        return [(128 * i // split[s], 128 * (i + 1) // split[s]) for i in range(split[s])]
+
+    def gather(name, s, win, winr, bias):
+        for a, b in parts(s):
+            li("%s_%d" % (name, a), ("g", 16 * (b - a)), [winr, ("o" + s, a, b)], [("g" + s, 16 * a, 16 * b)],
+               T["g" + s][:, 16 * a:16 * b], win.indirect(T["o" + s][:, a:b]), 1.0, bias)
+
+    def pick(i, s, src, w, dst, d0, bias):
+        gs = T["g" + src]
+        for a, b in parts(s):
+            tile, n = "%s%d_%d" % (s, i, a), b - a
+            gr = ("g" + src, 16 * a, 16 * b)
+            if i > 1 and s in turn:
+                m0 = 384 * w + 128 * (i - 2)
+                pe("t" + tile, 1024, [gr, ("sm", m0, m0 + 128)],
+                   lambda ps, a=a, b=b: [(ps[0:b - a, j:128:16], gs[:, 16 * a + j:16 * b:16], T.sm[:, m0 + 8 * j:m0 + 8 * j + 8], True, True) for j in range(16)])
+                tm = T["u" + s]
+                lp("d" + tile, "t" + tile, 0, 128, [], [("u" + s, 0, 128)], tm[0:n, :], p=n)
+                pe(tile, max(64, n), [("u" + s, 0, 128), ("idb", 0, 128)], lambda ps, n=n: [(ps[:, 0:n], tm[0:n, :], T.idb[0:n, 0:n], True, True)])
+            else:
+                pb, base = "pb%d" % (2 * w + (i - 1) // 2), 2048 * ((i - 1) % 2)
+                pe(tile, 16 * max(64, n), [gr, (pb, base, base + 2048)],
+                   lambda ps, a=a, b=b, pb=pb, base=base: [(ps[:, 0:b - a], T[pb][:, base + 128 * j:base + 128 * j + 128],
+                                                            gs[:, 16 * a + j:16 * b:16], j == 0, j == 15) for j in range(16)])
+            lp("c" + tile, tile, 0, n, [], [(dst, d0 + a, d0 + b)], T[dst][:, d0 + a:d0 + b], 1.0, bias)
+            if i == 4 and s in ("Yq", "Zr"):
+                u = 128 * (s == "Zr")
+                lp("e" + tile, tile, 0, n, [], [("dup", u + a, u + b)], T.dup[:, u + a:u + b])
+
+    def walk(s, src, w, dst, d0):
+        pick(1, s, src, w, "o" + s, 0, HALF)
+        gather("g" + s + "2", s, T.xi[:], XI, -HALF)
+        pick(2, s, s, w, "o" + s, 0, HALF)
+        gather("g" + s + "3", s, T.xi[:], XI, -HALF)
+        pick(3, s, s, w, "o" + s, 0, HALF)
+        gather("g" + s + "4", s, T.oi[:], OI, 0.0)
+        pick(4, s, s, w, dst, d0, 0.0)
+
+    def queries(t, s, width):
+        a, kl, ql = 128 * t, T.kl[:, 8 * t:8 * t + 8], T.ql[:, 8 * t:8 * t + 8]
+        tr, qr = ("t16", a, a + 128), ("ql", 8 * t, 8 * t + 8)
+        op("qc%d" % t, "V", ("g", 128), [("nxc", 0, width), ("kl", 8 * t, 8 * t + 8), ("qm", 0, 256)], [tr],
+           lambda e, ps: V.tensor_tensor(T.t16[:, a:a + 128], T.nxc[:, 0:width].indirect(kl), T.qm[:, a:a + 128], AL.mult))
+        pe("q%d" % t, 1024, [tr, ("w2", 0, 144)],
+           lambda ps: [(ps[:, 0:8], T.w2[:, 15 - r:143 - r], T.t16[:, a + r:a + 128:16], r == 0, r == 15) for r in range(16)])
+        lp("cq%d" % t, "q%d" % t, 0, 8, [], [qr], ql, 1.0, HALF)
+        li("s0" + s, ("g", 128), [XI, qr], [("o" + s, 0, 128)], T["o" + s][:], T.xi[:].indirect(ql))
+        gather("g" + s + "1", s, T.xi[:], XI, -HALF)
+
+    def match(t, qb, q0, rb, kc):
+        a = 128 * t
+        qr, qa = (qb, q0, q0 + 128), T[qb][:, q0:q0 + 128]
+        for h in range(2):
+            o = 256 * t + 128 * h
+            li("qh%d%d" % (t, h), ("ch", 128), [qr, pcr(7 + h)], [("qh", o, o + 128)], T.qh[:, o:o + 128], qa, col(7 + h), 0.0)
+        op("q2%d" % t, "A", ("c1", 128), [qr], [("q2", a, a + 128)], lambda e, ps: g.scalar.activation(T.q2[:, a:a + 128], qa, AF.Square))
+        op("r2%d" % t, "A", ("c1", kc), [(rb, 0, kc)], [("r2", a, a + kc)],
+           lambda e, ps: g.scalar.activation(T.r2[:, a:a + kc], T[rb][:, 0:kc], AF.Square))
+        for b in range(4):
+            tile = "m%d%d" % (t, b)
+
+            def seq(ps, p=slice(32 * b, 32 * b + 32)):
+                s = []
+                for h in range(2):
+                    out, eh = ps[:, kc * h:kc * h + kc], T.ee[p, 128 * h:128 * h + 128]
+                    s += [(out, eh, T.kv[p, 0:kc], True, False), (out, eh, T.r2[p, a:a + kc], False, False),
+                          (out, T.qh[p, 256 * t + 128 * h:256 * t + 128 * h + 128], T[rb][p, 0:kc], False, True)]
+                return s
+            pe(tile, 6 * kc, [("ee", 0, 256), ("kv", 0, 256), ("r2", a, a + kc), ("qh", 256 * t, 256 * t + 256), (rb, 0, kc)], seq)
+            for h in range(2):
+                j = 8 * t + 2 * b + h
+                op("rd%d" % j, "V", ("c1", kc), [], [("mn", j, j + 1)],
+                   lambda e, ps, j=j, h=h: V.tensor_reduce(T.mn[:, j:j + 1], ps[:, kc * h:kc * h + kc], AxisListType.X, AL.min), pr=tile)
+        tile = "k%d" % t
+        pe(tile, 640, [("mn", 8 * t, 8 * t + 8), ("idf", 0, 128), ("indk", 0, 8), ("q2", a, a + 128)],
+           lambda ps: [(ps[0:8, 0:128], T.indk[:], T.q2[:, a:a + 128], True, False),
+                       (ps[0:8, 0:128], T.mn[:, 8 * t:8 * t + 8], T.idf[:], False, True)])
+        nh, cum, tt = T.nh[0:8, a:a + 128], T.cum[0:8, a:a + 128], T.tt[0:8, a:a + 128]
+        nr, cr, tr, ones = ("nh", a, a + 128), ("cum", a, a + 128), ("tt", a, a + 128), ("rows", 256, 384)
+        op("nh%d" % t, "V", ("c1", 128), [], [nr], lambda e, ps: V.tensor_scalar(nh, ps[0:8, 0:128], 1024.0, -1.0, AL.is_lt, AL.mult), pr=tile)
+        own = T.ic[0:8, 128:256] if t == 0 else T.rows[0:8, 0:128]
+        l0 = 256 * t
+        op("cmp%d" % t, "V", ("c1", 128), [icr, ("rows", 0, 128)], [("ls", l0, l0 + 128)],
+           lambda e, ps: V.tensor_tensor(T.ls[0:8, l0:l0 + 128], ps[0:8, 0:128], own, AL.min), pr=tile)
+        init = 127.0 if t == 0 else T.cum[0:8, 127:128]
+        op("cum%d" % t, "V", ("c1", 128), [nr, ones, ("cum", 0, a)], [cr],
+           lambda e, ps: V.tensor_tensor_scan(cum, nh, T.rows[0:8, 256:384], init, AL.add, AL.add))
+        op("tt%d" % t, "V", ("c2", 128), [nr, ("rows", 128, 256)], [tr], lambda e, ps: V.tensor_tensor(tt, nh, T.rows[0:8, 128:256], AL.mult))
+        op("scl%d" % t, "V", ("c2", 128), [cr, tr], [("ls", l0 + 128, l0 + 256)],
+           lambda e, ps: V.tensor_tensor(T.ls[0:8, l0 + 128:l0 + 256], cum, tt, AL.max))
+        op("ym%d" % t, "V", ("c1", 128), [cr], [("yms", a, a + 128)],
+           lambda e, ps: V.tensor_tensor(T.yms[0:8, a:a + 128], ps[0:8, 0:128], cum, AL.min), pr=tile)
+
+        def lists(ps):
+            s = [(ps[:, 0:16], T.w1[0:8, 15 - r:143 - r], T.ls[0:8, l0 + r:l0 + 256:16], r == 0, r == 15) for r in range(16)]
+            if t == 0:
+                s += [(ps[:, 16:17], T.ind8[0:8, :], T.cum[0:8, 127:128], True, False),
+                      (ps[:, 16:17], T.ind8[0:8, :], T.rows[0:8, 256:257], False, True)]
+            return s
+        pe("l%d" % t, 1536 - 512 * t, [("w1", 0, 144), ("ls", l0, l0 + 256), ("ind8", 0, 128), cr, ones], lists)
+        lp("cl%d" % t, "l%d" % t, 0, 16, [], [("ll", 16 * t, 16 * t + 16)], T.ll[:, 16 * t:16 * t + 16])
+
+    def winner(t, wb, wn):
+        d0, w0, sd = 136 * t, 144 * t, T.sd[:, 16 * t:16 * t + 16]
+        op("dif%d" % t, "V", ("g", 128), [(wb, 0, wn), ("dup", 128 * t, 128 * t + 128), ("ll", 16 * t, 16 * t + 16)], [("df", d0, d0 + 128)],
+           lambda e, ps: V.tensor_tensor(T.df[:, d0:d0 + 128], T[wb][:, 0:wn].indirect(T.ll[:, 16 * t:16 * t + 8]),
+                                         T.dup[:, 128 * t:128 * t + 128], AL.not_equal))
+        sc, gm = T.sc[:, 2 * t:2 * t + 1], T.sc[:, 2 * t + 1:2 * t + 2]
+        sr, dr = ("sc", 2 * t, 2 * t + 1), ("sd", 16 * t, 16 * t + 16)
+        op("sco%d" % t, "V", ("c1", 129), [("df", d0, d0 + 129)], [sr], lambda e, ps: V.tensor_reduce(sc, T.df[:, d0:d0 + 129], AxisListType.X, AL.add))
+        li("sd%d" % t, ("c1", 16), [sr, ID], [dr], sd, T.id16[:], sc, 0.0)
+        pe("w%d" % t, 256, [("blk", 0, 128), dr], lambda ps: [(ps[:, 0:16], T.blk[:], sd, True, True)])
+        op("gm%d" % t, "V", ("c1", 16), [], [("sc", 2 * t + 1, 2 * t + 2)],
+           lambda e, ps: V.tensor_reduce(gm, ps[:, 0:16], AxisListType.X, AL.max), pr="w%d" % t)
+        a, b = (15, 143) if t == 0 else (0, 144)
+        ts("ww%d" % t, ("ch", b - a), [("w2", 0, 144), ("sc", 2 * t, 2 * t + 2)], [("ww", w0, w0 + 144)],
+           T.ww[:, w0 + a:w0 + b], T.w2[:, a:b], gm, sc, AL.mult, AL.is_equal)
+
+    li("s0b", ("g", 128), [TB, LU], [("ob", 0, 128)], T.ob[:], T.tb[:].indirect(T.lu[:, 0:8]), 1.0 / 16, RND)
+    li("nxb", ("g", 128), [TB, LU], [("nxc", 0, 128)], T.nxc[:, 0:128], T.tb[:].indirect(T.lu[:, 0:8]), 1.0 / 16, RND - HALF)
+    gather("gb1", "b", T.xi[:], XI, -HALF)
+    queries(0, "q", 128)
+    li("nxq", ("c1", 128), [("oq", 0, 128)], [("nxq", 0, 128)], T.nxq[:], T.oq[:], 1.0, -HALF)
+    walk("Eb", "b", 0, "rea", 0)
+    walk("Eq", "q", 0, "rea", 128)
+    walk("Yb", "b", 1, "ry", 0)
+    walk("Yq", "q", 1, "ry", 128)
+    walk("Zb", "b", 2, "zc", 0)
+    walk("Zq", "q", 2, "zq", 0)
+    scat("clr", 16, [SO, ("zsrc", 0, 1024)], "pb0", 0, 2048, T.so[:, 0:1], T.zsrc[:, 0:16])
+    match(0, "rea", 128, "rea", 128)
+    op("k1", "V", ("c1", 8), [("sf", 0, 8)], [("kl", 8, 16)],
+       lambda e, ps: V.tensor_scalar(T.kl[:, 8:16], T.sf[:], ps[:, 16:17], -0.5 + 2.0 ** -15, AL.mult, AL.add), pr="l0")
+    L0, L1 = ("ll", 0, 16), ("ll", 16, 32)
+    scat("snx", 128, [L0, ("nxq", 0, 128)], "nxc", 0, 512, T.ll[:, 8:16], T.nxq[:])
+    queries(1, "r", 256)
+    scat("szq", 128, [L0, ("zq", 0, 128)], "zc", 0, 512, T.ll[:, 8:16], T.zq[:])
+    winner(0, "ry", 256)
+    pe("u", 522, [("keep0", 0, 128), ("rea", 0, 261), ("ww", 0, 144), ("ry", 0, 261)],
+       lambda ps: [(ps[:, 0:261], T.keep0[:], T.rea[:, 0:261], True, False), (ps[:, 0:261], T.ww[:, 15:143], T.ry[:, 0:261], False, True)])
+    lp("elu", "u", 256, 261, [], [("elu", 0, 6)], T.elu[:, 0:5])
+    lp("so2", "u", 256, 257, [pcr(0)], [("so2", 0, 1)], T.so2[:, 0:1], 128.0, col(0))
+    lp("urc", "u", 0, 128, [], [("rc", 0, 128)], T.rc[:, 0:128])
+    lp("urt", "u", 128, 261, [], [("rt", 0, 136)], T.rt[:, 0:133])
+    li("vo2", ("g", 80), [("elu", 0, 6), ID], [("vo2", 0, 80)], T.vo2[:], T.id16[:].indirect(T.elu[:, 0:5]))
+    onehots("sq", 0, T.vo2, ("vo2", 0, 80), 0, T.so2, 0, ("so2", 0, 2))
+    scat("srt", 128, [L0, ("rt", 0, 136)], "rc", 0, 512, T.ll[:, 8:16], T.rt[:, 0:128])
+
+    walk("Er", "r", 0, "rq", 0)
+    walk("Zr", "r", 2, "zc", 512)
+    match(1, "rq", 0, "rc", 256)
+    dma("ymd", "S", 2.0, [("yms", 0, 256)], [("yd", 0, 1)], [(T.yd[:], T.yms[0:8, :])], "ymd")
+    scat("srq", 128, [L1, ("rq", 0, 128)], "rc", 0, 512, T.ll[:, 24:32], T.rq[:])
+    send("rc", 0.5, 3.5, ("rc", 0, 384), ("rcl", 0, 384), T.rcl[:], T.rc[:, 0:384])
+    send("ym", 0.5, 2.0, ("yd", 0, 1), ("yl", 0, 1), T.yl[:], T.yd[:])
+    li("rcf", ("ch", 384), [("rcl", 0, 384)], [("rcf", 0, 384)], T.rcf[:], T.rcl[:])
+    dma("oyr", "S", 2.6, [("rcf", 0, 384)], [("yr", 0, 1)], [(T.yr[:], T.rcf[:])], "oyr")
+    dma("oym", "S", 2.0, [("yl", 0, 1)], [("ym", 0, 1)], [(T.ym[:], T.yl[:])], "oym")
+    winner(1, "zc", 640)
+    scat("szr", 128, [L1, ("zc", 512, 640)], "zc", 0, 512, T.ll[:, 24:32], T.zc[:, 512:640])
+    pe("f", 1152, [("ww", 144, 288), ("zc", 0, 645), ("keep1", 0, 128), ("rt", 0, 136)],
+       lambda ps: [(ps[:, 0:24], T.ww[:, 159 - r:287 - r], T.zc[:, 24 * r:24 * r + 24], r == 0, r == 15) for r in range(16)]
+       + [(ps[:, 24:29], T.keep1[:], T.rt[:, 128:133], True, False), (ps[:, 24:29], T.ww[:, 158:286], T.zc[:, 640:645], False, True)])
+    lp("fin", "f", 0, 29, [], [("fin", 0, 29)], T.fin[:])
+    send("fin", 0.5, 2.5, ("fin", 0, 29), ("finl", 0, 29), T.finl[:], T.fin[:])
+    dma("ofin", "S", 2.0, [("finl", 0, 29)], [("yr", 0, 1)], [(T.yr[1::16, :], T.finl[:, 0:24])], "ofin")
+    dma("oye", "A", 2.0, [("finl", 0, 29)], [("ye", 0, 1)], [(T.ye[:], T.finl[:, 24:29])], "ofin")
+    return ops
+
+
+def data_deps(ops):
+    by, tiles, deps = {}, {}, {}
+    for o in ops:
+        acc = [("r",) + x for x in o["r"]] + [("w",) + x for x in o["w"]]
+        d = set(n2 for kind, b, lo, hi in acc for k2, l2, h2, n2 in by.get(b, []) if "w" in (kind, k2) and lo < h2 and l2 < hi)
+        for kind, b, lo, hi in acc:
+            by.setdefault(b, []).append((kind, lo, hi, o["n"]))
+        if o["pw"]:
+            tiles[o["pw"]] = o["n"]
+        if o["pr"]:
+            d.add(tiles[o["pr"]])
+        deps[o["n"]] = d
+    return deps
+
+
+def parse(text, ops):
+    v = [int(text[i:i + 2], 36) for i in range(0, len(text), 2)]
+    assert sorted(x // 2 for x in v) == list(range(len(ops)))
+    return [(ops[x // 2], ops[x // 2]["e"][x % 2]) for x in v]
+
+
+def emit(g, T, ops, order):
+    Q = {"V": g.vector, "A": g.scalar, "P": g.tensor, "G": g, "S": g.sync}
+    deps = data_deps(ops)
+    left = {}
+    for o in ops:
+        left[o["pr"]] = left.get(o["pr"], 0) + 1
+    free, bank_of, users = list(range(NB)), {}, {}
+    chan, seq, know, done, plan, needed = {}, {}, {k: {} for k in Q}, {}, [], set()
+    for o, e in order:
+        n, b = o["n"], None
+        d = set(deps[n])
+        if o["pw"]:
+            b = bank_of[o["pw"]] = free.pop(0)
+            d |= set(users.get(b, []))
+            users[b] = []
+        if o["pr"]:
+            b = bank_of[o["pr"]]
+            d |= set(u for u in users[b] if chan[u][0] != "c" + e)
+            users[b].append(n)
+            left[o["pr"]] -= 1
+            if left[o["pr"]] == 0:
+                free.append(b)
+        seq[e] = seq.get(e, 0) + 1
+        chan[n] = (o["sem"][0], 1) if o["sem"] else ("c" + e, seq[e])
+        waits, done[n] = [], {}
+        if e != "X":
+            k = know[e]
+            for x in sorted(d, key=lambda x: (-chan[x][1], x)):
+                if k.get(chan[x][0], 0) < chan[x][1]:
+                    waits.append(x)
+                    needed.add(x)
+                    for c2, v2 in done[x].items():
+                        k[c2] = max(k.get(c2, 0), v2)
+            done[n] = dict(k)
+        done[n][chan[n][0]] = chan[n][1]
+        plan.append((o, e, b, waits))
+    count, val, total, waited = {}, {}, {}, set()
+    for o, e, b, waits in plan:
+        if o["sem"]:
+            total[o["sem"][0]] = total.get(o["sem"][0], 0) + o["sem"][1]
+            val[o["n"]] = o["sem"][1]
+        elif o["n"] in needed:
+            count[e] = val[o["n"]] = count.get(e, 0) + 1
+    for o, e, b, waits in plan:
+        if e == "X":
+            continue
+        for x in waits:
+            Q[e].wait_ge(T.sem[chan[x][0]], val[x])
+            waited.add(chan[x][0])
+        ins = o["f"](e, None if b is None else T["ps%d" % b])
+        if o["sem"]:
+            for i in (ins if e != "G" else []):
+                i.then_inc(T.sem[o["sem"][0]], 16)
+        elif o["n"] in needed:
+            ins.then_inc(T.sem["c" + e], 1)
+    for s, v in total.items():
+        if s not in waited:
+            Q["G" if s == "lsem" else "S"].wait_ge(T.sem[s], v)
+
+
+def rank_program(g, core, T, topo):
+    rank = T.rank_of(core)
+    if rank is None:
+        return
+    n = len(T.cores)
+    other = T.cores[(rank + n // 2) % n]
+    rid, pid = topo.addr(other, core)
+    ops = make_ops(g, T, (rid, pid, topo.mask(core, other), len(topo.engines(core, other))), CFG)
+    emit(g, T, ops, parse(ORDER, ops))

@@ -4,404 +4,382 @@ AL = AluOpType
 AF = ActivationFunctionType
 C = 3072
 HALF = 1536.0
-CH = [0, 1024, 2048, 2816, 3072]
-STREAMS = ["b", "q", "r", "Eb", "Eq", "Yb", "Yq", "Zb", "Zq", "Er", "Zr"]
-CFG = {"split": {k: 1 if k in ("Yb", "Yq", "Zb", "Zq") else 2 for k in STREAMS}, "turn": []}
-ORDER = ("00020406080m0s0g0a1a16180c2q1c2e1s1e1g1o0e1k1q24302k2a2m0o0r101u1y0v222t0i0k2h34202x122z281w1m382c3i33373k3b3t4c4e3e0w4h3g1i"
-         "4k4m143m3o4p4r4v3q404y4i526a50574s6654596c446g9w80685a826e3c5e5g857e7g7j6m6i5k8646425q6o5c6k6t888b7k6q6u5t0y488o9a5i5m7m8r8t"
-         "6y6w7o727q708c7t5o5v5x748e768u7u7a7d79a15y61627w8g65a49zaiak8xa6aaama89daoasaqacag3vaea2au264a2uawb02pb2ayb44w7y8i8kb88m3x9f"
-         "ba9gbcbebgbi8zbubwbybkbnc0c29ibrc490c6bo9lc8cacgci92ceckdwcccmcocqcscucwdye4e0czd0d4d69me2dad3d9dcdedkdge7e8eadjdneceg9pfedo"
-         "drdsdufbekf8efen9qfcfyg0fmfqejetfgfofsfifk95eoewg2fwfueqev2ig49s9vg6gcga3zg8gef0gigkgogqggezb69698bsgsf2f4gmguf6h4h6h9hghahc"
-         "hehihkhmgwgyh0h2hohqhs")
+RND = -0.46875
+CFG = {"chunks": [0, 1024, 2048, 2688, 3072],
+       "cut": {"b": 2, "q": 2, "r": 2, "Eb": 2, "Eq": 2, "Er": 2, "Yb": 2, "Yq": 2, "Zb": 2, "Zq": 2, "Zr": 2},
+       "order": "000c0o020e0406080a0g0i24260s280q0k2a3g2s102e2q2k2w3q2m3i2h2j2o3n3a2d3c3l2v2y3t3p383e3v3w303632343z401243440m0u47480w0y1416181a1c1e1g1i1k1m1o1q1s1u1w1y20224b4h4d57595b4q4k4i5e5g5c5j4n4u5w5l5n5s5z5o5v704w634y9g7473604o889j796876647a7c9o7g667e7i6b8b6f8c8h8e9k9s8k6k6c9n6g507l7m7o8j9u527r6i7s7v7x7z5rao8obw8m6m6o6s6qby6w80846u8sa16y82da87d68wd9du9qdc8rdedw4edmdodg8ya4are0dqe2eadke48vdydia7e8959w90dse69yeca2egeu98ada8eeei92ekf04teqemag9aabf2f4979caef6axajeof9akc49easb0amavc8fgfb54fifkfmb2d4c0fofqcbfsfufwesg0hgg2g8fyg4g6fdb9gcikgac2gfgggjexiigkaygoc7gmhkgqhnb4gscciogvgwcghjhrh0bcj4gyceh2h7hwh4hcb7bfhoh8jcigiwbbhehbiyj6hzciiqimezj0j2j8ckisjeiujahsi3cnbgbljghvjii8cojkcsjmibcrbojqbijocuk0jsi1bnjuk2ifi4cwi6brk4d0k6bscyjwbvksd3jzkxicfekkk8kukmkokqkyl1l8l2l4l6kblakelckclelgkhlikilk",
+       "lead": {"Eb": 4.5, "Eq": 4, "Er": -2, "Zr": 1, "Zq": 2.5, "Yb": 2, "Zb": 1}, "gather": 1.3, "scatter": 3.2, "hop": 0.15, "pe": 0.42,
+       "inp": 7.5, "lean": 0.8, "early": 1.5, "passes": 1, "fix": 0.06}
+CFG["order"] = "000c0o020e0406080a0g0i24260s280q0k2a3g2s102e2q2k2w3q2m3i2h2j2o3n3a2d3c3l2v2y3t3p383e3v3w303632343z401243440m0u47480w0y1416181a1c1e1g1i1k1m1o1q1s1u1w1y20224b4c4h594l564i5b5e4u5g5j5l5s5c5o5w4q4n5y4y745v5n70614s7773629g4w68648c9i787b9o676b7c6d6f50888e9k7e8a7g6g7j8h6k7k6n6i7o9s8j7m8k7s8o7q6o6s8n528s7u5q6rao9u8r7x6w6u7y8w6y9mbwa18084daaq82a4d887d69ra7d4dm8z8udodedqdge2e4dudwdsdie6dk9w4fdye0dce89yadeaee9590eca2egag4peia8as92abbyaj96euaff098ek9ceqemax9a9eepakf2c4f4aub0anfgfic0f7fkc2f9fbfmc8fob2fqescafs54hgfufdfwfyg0g2c6gcgeg8b9gbccaycebcgjhkg6b4bfgoghexcghmgqhjikgkg4eycjhpjciwb7guckgmh0coiggshqh3hsgwcnblh7bbj4bogyhwiicqh4cuhzhchvh8ioi2hfhbi1imiyjebgi8j6j0j2bictjiibiqjgjaiubnj8jkd0isi4cwjmk0joi7d2jqjucziebrbsbuk2jwjsidfejzksk4klk6kukxkmkokqk8kyl1l2l8l4l6lalckbkclekelgkhkililk"
 NB = 8
 F32, BF, F16, I32, U16 = "float32", "bfloat16", "float16", "int32", "uint16"
 SB = {"snd": (55, I32), "inp": (55, I32), "lu": (56, U16), "tb": (C, I32), "xi": (C, I32), "oi": (C, I32),
-      "ic": (256, F32), "cd": (128, F32), "jc": (12, F32), "ri": (4, I32), "pc": (16, F32),
-      "id16": (16, BF), "w2": (144, BF), "w1": (144, F16), "blk": (128, F32), "ind8": (128, F32), "indk": (8, BF),
-      "idf": (128, F32), "idb": (128, BF), "keep0": (128, BF), "keep1": (128, BF), "ee": (256, BF), "kv": (256, BF),
-      "rows": (384, F32), "zsrc": (1024, BF), "so": (12, U16), "so2": (2, U16), "st": (4, U16), "sm": (1152, BF),
-      "vo": (240, BF), "vo2": (80, BF), "elu": (6, U16), "qm": (256, BF), "kl": (16, U16), "sf": (8, F32),
-      "nxc": (512, I32), "nxq": (128, I32), "t16": (256, F16), "ql": (16, U16), "dup": (256, BF),
-      "rea": (264, BF), "ry": (264, BF), "zc": (648, BF), "zq": (128, BF), "rc": (512, BF), "rq": (128, BF), "rt": (136, BF),
-      "qh": (512, BF), "q2": (256, BF), "r2": (384, BF), "mn": (16, F32), "nh": (256, F32), "cum": (256, F32),
-      "tt": (256, F32), "ls": (512, F16), "yms": (256, F32), "ll": (32, U16), "df": (272, BF), "sc": (4, F32), "sd": (32, F32),
-      "ww": (288, BF), "fin": (29, F32), "finl": (29, F32), "rcl": (384, BF), "rcf": (384, F32)}
-for _k in range(6):
-    SB["pb%d" % _k] = (4096, BF)
+      "ic": (256, F32), "cd": (128, F32), "jc": (12, F32), "ri": (4, I32), "pc": (16, F32), "one": (128, BF), "cst": (32, BF),
+      "id16": (16, BF), "w2": (144, BF), "wa": (144, BF), "blk": (128, BF), "indk": (8, BF), "idb": (128, BF), "keep0": (128, BF), "keep1": (128, BF),
+      "ee": (256, BF), "kv": (768, BF), "tri": (128, F16), "dg": (128, F16), "mx": (144, F16), "zsrc": (2048, BF),
+      "so": (12, U16), "so2": (2, U16), "vo": (240, BF), "vo2": (80, BF), "elu": (6, U16), "qm": (256, BF), "kl": (16, U16), "sf": (8, F32),
+      "nxc": (656, I32), "nxq": (128, I32), "t16": (256, F16), "ql": (16, U16), "pb": (12 * 2048, BF),
+      "rea": (272, BF), "ry": (288, BF), "zc": (656, BF), "zq": (128, BF), "zr": (136, BF), "zm": (128, BF), "rc": (800, BF), "rq": (128, BF),
+      "rm": (768, BF), "q2": (256, BF), "r2": (384, BF), "mn": (16, F32), "md": (16, F32), "nw": (288, BF), "ms": (288, BF),
+      "ll": (32, U16), "df": (272, BF), "sc": (4, F32), "sd": (32, F16), "ww": (288, BF), "fin": (29, F32), "finl": (29, F32),
+      "rcl": (400, BF), "rcf": (384, F32), "ymf": (256, F32)}
+STREAMS = ["b", "q", "r", "Eb", "Eq", "Yb", "Yq", "Zb", "Zq", "Er", "Zr"]
 for _k in STREAMS:
     SB["g" + _k] = (2048, F16)
     SB["o" + _k] = (128, U16)
-    SB["u" + _k] = (128, F16)
 SCRATCH = {k: ("sbuf", [128, v[0]], v[1]) for k, v in SB.items()}
-SCRATCH["yd"] = ("dram", [128, 16], F32)
-SCRATCH["yl"] = ("dram", [128, 16], F32)
 for _k in range(NB):
     SCRATCH["ps%d" % _k] = ("psum", [128, 512], F32)
-SEMAPHORES = ["cV", "cA", "cP", "cG", "ldin", "tb0", "tb1", "tb2", "tb3", "z1", "z3", "z5", "ymd", "oym", "oyr", "ofin",
-              "lsem", "ainp", "aym", "arc", "afin"]
+SEMAPHORES = ["cV", "cA", "cP", "cG", "ld0", "ld1", "tb0", "tb1", "tb2", "tb3", "zf0", "zf1", "zf2", "oym", "oyr", "ofin", "oye",
+              "linp", "lrc", "lfin", "ainp", "arc", "afin"]
+R0 = 144
 
 
-def make_ops(g, T, peer, cfg):
+def v(buf, a=0, b=None, step=1, p=(0, 128)):
+    return ("s", buf, a, SB[buf][0] if b is None else b, step, p)
+
+
+def ps(tile, a, b, p=(0, 128)):
+    return ("p", tile, a, b, 1, p)
+
+
+def at(win, off):
+    return ("i", win, off)
+
+
+def col(j):
+    return v("pc", j, j + 1)
+
+
+def spans(x):
+    if not isinstance(x, tuple):
+        return []
+    return spans(x[1]) + spans(x[2]) if x[0] == "i" else [x[:4]]
+
+
+def size(x):
+    return 16 * size(x[2]) if x[0] == "i" else (x[3] - x[2] + x[4] - 1) // x[4]
+
+
+def make_ops(cfg):
     ops = []
-    rid, pid, mask, nen = peer
-    split, turn = cfg["split"], cfg["turn"]
-    V = g.vector
-    Q = {"A": g.scalar, "S": g.sync}
-    sets = [("Eb", "Eq", "Er"), ("Yb", "Yq"), ("Zb", "Zq", "Zr")]
-    need_t = [any(s in turn for s in w) for w in sets]
-    need_d = [any(s not in turn for s in w) for w in sets]
+    cyc = 0.00083
 
-    def op(name, eng, cost, r, w, fn, pw=None, pr=None, sem=None):
-        ops.append({"n": name, "e": eng, "c": cost, "r": r, "w": w, "f": fn, "pw": pw, "pr": pr, "sem": sem})
+    def narrow(x):
+        return x[0] == "s" and SB[x[1]][1] in (BF, F16, U16)
 
-    def lin(e, out, in_, scale=1.0, bias=0.0):
-        if e == "V":
-            return V.tensor_scalar(out, in_, scale, bias, AL.mult, AL.add)
-        return g.scalar.activation(out, in_, AF.Copy if isinstance(bias, float) else AF.Identity, bias=bias, scale=scale)
+    def op(name, eng, calls, cost=None, r=(), w=(), sem=None, late=0.0):
+        rd, wt = list(r), list(w)
+        for m, a in calls:
+            out = a[0][1] if a[0][0] == "i" else a[0]
+            wt += spans(out)
+            rd += [s for x in a[1:] for s in spans(x)] + (spans(a[0][2]) if a[0][0] == "i" else [])
+        if cost is None:
+            m, a = calls[0]
+            if m == "matmul":
+                cost = sum(max(min(64, size(a[1])), size(a[2])) for m, a in calls) * cfg["pe"] / 1000
+            elif m == "iota":
+                cost = 0.13 + 2 * cyc * size(a[0])
+            elif a[0][0] == "i":
+                cost = 0.05 + size(a[0]) * cfg["scatter"] / 1000
+            elif isinstance(a[1], tuple) and a[1][0] == "i":
+                cost = 0.06 + size(a[1]) * cfg["gather"] / 1000
+            else:
+                n = size(a[0] if m == "memset" else a[1])
+                half = m in ("memset", "tensor_scalar", "lin") and narrow(a[0]) and (m == "memset" or narrow(a[1]))
+                two = m == "tensor_tensor" and a[1][0] == a[2][0]
+                cost = {e: cfg["fix"] + cyc * n * (0.5 if half and e == "V" else 2 if two else 1) for e in eng}
+        ops.append({"n": name, "e": eng, "calls": calls, "c": cost if isinstance(cost, dict) else {e: cost for e in eng},
+                    "r": rd, "w": wt, "sem": sem, "late": late})
 
-    def col(j):
-        return T.pc[:, j:j + 1]
+    def lin(name, out, in_, scale=1.0, bias=0.0, eng="VA"):
+        op(name, eng, [("lin", (out, in_, scale, bias))])
 
-    def pcr(j):
-        return ("pc", j, j + 1)
+    def ts(name, out, in0, s1, s2, *o):
+        op(name, "V", [("tensor_scalar", (out, in0, s1, s2) + o)])
 
-    def ts(name, cost, r, w, out, in0, s1, s2, *o):
-        op(name, "V", cost, r, w, lambda e, ps: V.tensor_scalar(out, in0, s1, s2, *o))
+    def tt(name, out, a, b, o):
+        op(name, "V", [("tensor_tensor", (out, a, b, o))])
 
-    def eq(buf, n, src, j, p=128):
-        ts(buf, ("c1", n), [(src, 0, n), pcr(j)], [(buf, 0, n)], T[buf][0:p, 0:n], T[src][0:p, 0:n], T.pc[0:p, j:j + 1], None, AL.is_equal)
+    def red(name, out, in_, o):
+        op(name, "V", [("tensor_reduce", (out, in_, AxisListType.X, o))])
 
-    def li(name, cost, r, w, out, in_, scale=1.0, bias=0.0, eng="VA"):
-        op(name, eng, cost, r, w, lambda e, ps: lin(e, out, in_, scale, bias))
+    def eq(buf, src, j):
+        ts(buf, v(buf), v(src, 0, SB[buf][0]), col(j), None, AL.is_equal)
 
-    def lp(name, tile, a, b, r, w, out, scale=1.0, bias=0.0, p=128):
-        op(name, "VA", ("c1", b - a), r, w, lambda e, ps: lin(e, out, ps[0:p, a:b], scale, bias), pr=tile)
+    def fill(name, x, val):
+        op(name, "V", [("memset", (x, val))])
 
-    def fill(name, buf, a, b, val, kind="ch"):
-        def f(e, ps):
-            if e == "V":
-                return V.memset(T[buf][:, a:b], val)
-            return lin(e, T[buf][:, a:b], T.zsrc[:, 0:b - a], 0.0, float(val))
-        op(name, "VA", (kind, b - a), [("zsrc", 0, 1024)], [(buf, a, b)], f)
+    def scat(name, win, off, src):
+        op(name, "V", [("tensor_copy", (at(win, off), src))])
 
-    def dma(name, q, t, r, w, pairs, sem):
-        op(name, q, ("dma", t), r, w, lambda e, ps: [Q[e].dma_start(o, i) for o, i in pairs], sem=(sem, 16 * len(pairs)))
+    def pe(name, seq, last=True):
+        op(name, "P", [("matmul", (o, l, r, s, last and t)) for o, l, r, s, t in seq])
 
-    def send(name, t0, t1, r, w, out, in_):
-        op("s" + name, "G", ("rem", t0), [r], [("x" + name, 0, 1)],
-           lambda e, ps: g.remote_dma(out, in_, T.sem["a" + name], T.sem.lsem, pid, rid, mask), sem=("lsem", nen))
-        op("a" + name, "X", ("arr", t1), [("x" + name, 0, 1)], [w], None, sem=("a" + name, nen))
+    def acc(out, terms):
+        return [(out, l, r, i == 0, i == len(terms) - 1) for i, (l, r) in enumerate(terms)]
 
-    def pe(name, n, r, seq):
-        def f(e, ps):
-            last = None
-            for out, l, rr, st, sp in seq(ps):
-                last = g.tensor.matmul(out, l, rr, st, sp)
-            return last
-        op("p" + name, "P", ("pe", n), r, [], f, pw=name)
+    def iota(x, pat, cm=0, base=0):
+        op("i%s%d" % x[1:3], "G", [("iota", (x, pat, base, cm))])
 
-    def iota(buf, n, pat):
-        op("i" + buf, "G", ("io", n), [], [(buf, 0, n)], lambda e, ps: g.iota(T[buf][:, 0:n], pat, 0, 0, allow_small_or_imprecise_dtypes=True))
+    def hbm(name, idx):
+        return ("d", name, 0, 1, idx)
 
-    def scat(name, n, r, wbuf, a, b, offs, src):
-        op(name, "V", ("s", n), r, [(wbuf, a, b)], lambda e, ps: V.tensor_copy(T[wbuf][:, a:b].indirect(offs), src))
+    def dma(name, q, t, pairs, r=()):
+        op(name, q, [("dma_start", x) for x in pairs], 0.06 * len(pairs), r=r, sem=name, late=t)
 
-    dma("ldin", "S", 2.2, [], [("snd", 0, 55)], [(T.snd[:, 0:8], T.bk[:]), (T.snd[:, 40:45], T.ex[:]), (T.snd[:, 45:55], T.zs[:]),
-                                                 (T.snd[:, 8:24], T.qs[:]), (T.snd[:, 24:40], T.qc[:])], "ldin")
-    for k in range(4):
+    def send(name, t0, t1, out, in_):
+        op("l" + name, "G", [("remote_dma", (("x", name, 0, 1, out), in_))], 0.3, sem="l" + name, late=t0)
+        op("a" + name, "X", [], 0.0, r=[("x", name, 0, 1)], w=spans(out), sem="a" + name, late=t1)
+
+    ALL = slice(None)
+
+    dma("ld0", "S", 1.6, [(v("snd", 0, 8), hbm("bk", ALL)), (v("snd", 8, 24), hbm("qs", ALL)), (v("snd", 24, 40), hbm("qc", ALL))])
+    dma("ld1", "A", 1.6, [(v("snd", 40, 45), hbm("ex", ALL)), (v("snd", 45, 55), hbm("zs", ALL))])
+    CH = cfg["chunks"]
+    for k in range(len(CH) - 1):
         a, b = CH[k], CH[k + 1]
-        dma("tb%d" % k, "A", 2.5 + 5.0 * b / C, [], [("tb", a, b)], [(T.tb[:, a:b], T.mt[:, a:b])], "tb%d" % k)
-    op("ri0", "G", ("io", 1), [], [("ri", 0, 1)], lambda e, ps: g.iota(T.ri[:, 0:1], [[0, 1]], 0, 1))
-    iota("ic", 256, [[1, 256]])
-    iota("jc", 12, [[0, 3], [0, 2], [2048, 2]])
-    iota("cd", 128, [[1, 8], [0, 16]])
-    INP = ("inp", 0, 55)
-    send("inp", 1.0, 4.0, ("snd", 0, 55), INP, T.inp[:], T.snd[:])
+        dma("tb%d" % k, "S", 1.8 + 4.5 * b / C, [(v("tb", a, b), hbm("mt", (ALL, slice(a, b))))])
+    iota(v("ri", 0, 1), [[0, 1]], 1)
+    iota(v("ic"), [[1, 256]])
+    iota(v("jc"), [[0, 3], [0, 2], [2048, 2]])
+    iota(v("cd"), [[1, 8], [0, 16]])
+    send("inp", cfg["inp"] - 3.5, 1.0, v("inp"), v("snd"))
 
-    wid = [4096 if d else 2048 for d in need_d]
-    op("zsrc", "V", ("ch", 1024), [], [("zsrc", 0, 1024)], lambda e, ps: V.memset(T.zsrc[:], 0.0))
-    for k in range(wid[0] // 1024):
-        fill("zp0_%d" % k, "pb0", 1024 * k, 1024 * k + 1024, 0.0)
-    iota("pb2", wid[1], [[0, wid[1]]])
-    iota("pb4", wid[2], [[0, wid[2]]])
-    n = 0
-    for w in range(3):
-        if need_d[w]:
-            b = "pb%d" % (2 * w + 1)
-            dma("z" + b, "S", 5.0 + 4.0 * n, [("zsrc", 0, 1024), ("tb", 0, C)], [(b, 0, 4096)],
-                [(T[b][:, 1024 * j:1024 * j + 1024], T.zsrc[:]) for j in range(4)], "z%d" % (2 * w + 1))
-            n += 1
-        if need_t[w]:
-            fill("zsm%d" % w, "sm", 384 * w, 384 * w + 384, 0.0)
+    def pbv(k, n=1):
+        return v("pb", 2048 * k, 2048 * (k + n))
+    fill("zsrc", v("zsrc"), 0.0)
+    fill("zp0", pbv(0), 0.0)
+    lin("zp1", pbv(1), v("zsrc"), 0.0, 0.0, "A")
+    for j in range(3):
+        dma("zf%d" % j, "S", 3.5 + 3.3 * j, [(pbv(4 + 2 * j + i), v("zsrc")) for i in range(2)], r=[("x", "inp", 0, 1), ("s", "tb", 0, C)])
+
+    def const(x, c):
+        iota(x, [[0, size(x)]], base=c)
+
+    const(pbv(2), 0)
+    const(pbv(3), 0)
+    iota(v("kv", 0, 256), [[0, 2], [1, 128]])
+    const(v("one"), 1)
+    iota(v("cst", 0, 8), [[-1, 8]])
+    iota(v("cst", 8, 24), [[8, 2], [0, 8]], base=8)
+    for x, c in ((v("cst", 24, 32), -8), (v("nw"), 0), (v("ms"), 0), (v("nxc", 128, 256), 0), (v("rea", 133, 144), 0), (v("ry", 133, 144), 0),
+                 (v("ry", 272, 288), -1), (v("df", 129, 130), -64), (v("df", 265, 266), -64),
+                 (v("rc", R0 + 128, R0 + 384), -1), (v("zc", 128, 384), -1)):
+        const(x, c)
+    iota(v("kv", 256, 768), [[0, 2], [1, 256]])
+    const(pbv(10), 0)
+    const(pbv(11), 0)
 
     for j, (c, o) in enumerate(((15, AL.bitwise_and), (4, AL.arith_shift_right), (16, AL.bitwise_and))):
-        ts("ri%d" % (j + 1), ("c1", 1), [("ri", 0, 1)], [("ri", j + 1, j + 2)], T.ri[:, j + 1:j + 2], T.ri[:, 0:1], c, None, o)
-    li("pc0", ("c1", 4), [("ri", 0, 4)], [("pc", 0, 4)], T.pc[:, 0:4], T.ri[:])
-    for j, src, sc, bi in ((4, 0, 16.0, 15.0), (6, 2, 16.0, 15.0), (7, 3, 128.0, -2048.0), (8, 3, -128.0, 0.0), (9, 3, -64.0, 1024.0), (10, 3, 64.0, 0.0)):
-        li("pc%d" % j, ("c1", 1), [pcr(src)], [pcr(j)], col(j), col(src), sc, bi)
-    li("pc5", ("c1", 1), [pcr(0), pcr(1)], [pcr(5)], col(5), col(1), 128.0, col(0))
-    icr = ("ic", 0, 256)
-    eq("id16", 16, "ic", 1)
-    li("pc11", ("c1", 2), [("id16", 0, 16), pcr(0)], [("pc", 11, 13)], T.pc[:, 11:13], T.id16[:, 0:2], -1000.0, col(0))
-    eq("w2", 144, "ic", 6)
-    eq("w1", 144, "ic", 4, 8)
-    eq("blk", 128, "cd", 2)
-    eq("ind8", 128, "cd", 0, 8)
-    eq("idf", 128, "ic", 0)
-    eq("keep0", 128, "ic", 11)
-    eq("keep1", 128, "ic", 12)
-    ts("indk", ("c1", 8), [icr, pcr(2)], [("indk", 0, 8)], T.indk[:], T.ic[:, 0:8], col(2), 1024.0, AL.is_equal, AL.mult)
-    if turn:
-        eq("idb", 128, "ic", 0)
-        li("pc13", ("c1", 1), [pcr(1), pcr(2)], [pcr(13)], col(13), col(1), 8.0, col(2))
-        li("st", ("c1", 3), [icr, pcr(13)], [("st", 0, 4)], T.st[:, 0:3], T.ic[:, 0:3], 128.0, col(13))
+        ts("ri%d" % (j + 1), v("ri", j + 1, j + 2), v("ri", 0, 1), c, None, o)
+    lin("pc0", v("pc", 0, 4), v("ri"))
+    for j, src, sc, bi in ((4, 1, -1.0, 527.0), (6, 2, 16.0, 15.0), (7, 3, 128.0, -2048.0), (8, 3, -128.0, 0.0), (9, 3, -64.0, 1024.0),
+                           (10, 3, 64.0, 0.0), (13, 0, 1.0, -399.0)):
+        lin("pc%d" % j, col(j), col(src), sc, bi)
+    lin("pc5", col(5), col(1), 128.0, col(0))
+    eq("id16", "ic", 1)
+    lin("pc11", v("pc", 11, 13), v("id16", 0, 2), -1000.0, col(0))
+    for buf, src, j in (("w2", "ic", 6), ("blk", "cd", 2), ("idb", "ic", 0), ("keep0", "ic", 11), ("keep1", "ic", 12)):
+        eq(buf, src, j)
+    ts("wa", v("wa"), v("ic", 0, 144), col(6), 1000.0, AL.not_equal, AL.mult)
+    ts("indk", v("indk"), v("ic", 0, 8), col(2), -1024.0, AL.is_equal, AL.mult)
+    ts("tri", v("tri"), v("ic", 0, 128), col(0), None, AL.is_gt)
+    ts("dg", v("dg"), v("ic", 0, 128), col(0), col(13), AL.is_equal, AL.mult)
+    tt("mx", v("mx", 0, 128), v("tri"), v("dg"), AL.add)
+    lin("mx1", v("mx", 128, 144), v("zsrc", 0, 16), 0.0, 1.0)
     for h in range(2):
-        li("ee%d" % h, ("c1", 128), [icr, pcr(9 + h)], [("ee", 128 * h, 128 * h + 128)], T.ee[:, 128 * h:128 * h + 128], T.ic[:, 0:128], 0.0, col(9 + h))
-        li("dfc%d" % h, ("c1", 1), [pcr(1)], [("df", 136 * h + 128, 136 * h + 129)], T.df[:, 136 * h + 128:136 * h + 129], col(1), -1.0 / 16, 1.0)
-    li("kv", ("c1", 256), [icr], [("kv", 0, 256)], T.kv[:], T.ic[:], 2.0 ** -14, 0.0)
-    for j, (sc, bi) in enumerate(((1.0, 512.0), (-1.0, -384.0), (0.0, 1.0))):
-        li("row%d" % j, ("c1", 128), [icr], [("rows", 128 * j, 128 * j + 128)], T.rows[0:8, 128 * j:128 * j + 128], T.ic[0:8, 0:128], sc, bi)
-    fill("frc", "rc", 128, 512, -1.0)
-    fill("fzc", "zc", 128, 512, -1.0)
-    fill("fnx", "nxc", 128, 256, 0, "c1")
-    li("soc", ("c1", 12), [("jc", 0, 12), pcr(5)], [("so", 0, 12)], T.so[:], T.jc[:], 1.0, col(5))
-    li("so2c", ("c1", 1), [pcr(5)], [("so2", 1, 2)], T.so2[:, 1:2], col(5), 1.0, 2048.0)
+        lin("ee%d" % h, v("ee", 128 * h, 128 * h + 128), v("zsrc", 0, 128), 0.0, col(9 + h))
+        lin("dfc%d" % h, v("df", 136 * h + 128, 136 * h + 129), col(1), -1.0 / 16, 0.0)
+    lin("soc", v("so"), v("jc"), 1.0, col(5))
+    lin("so2c", v("so2", 1, 2), col(5), 1.0, 2048.0)
 
-    RND = -0.46875
-    for k in range(4):
+    for k in range(len(CH) - 1):
         a, b = CH[k], CH[k + 1]
-        li("x%d" % k, ("c1", b - a), [("tb", a, b)], [("xi", a, b)], T.xi[:, a:b], T.tb[:, a:b], 1.0 / 16, RND)
-        ts("o%d" % k, ("c1", b - a), [("tb", a, b)], [("oi", a, b)], T.oi[:, a:b], T.tb[:, a:b], 15, None, AL.bitwise_and)
-    XI, OI, TB = ("xi", 0, C), ("oi", 0, C), ("tb", 0, C)
+        lin("x%d" % k, v("xi", a, b), v("tb", a, b), 1.0 / 16, RND)
+        ts("o%d" % k, v("oi", a, b), v("tb", a, b), 15, None, AL.bitwise_and)
 
-    LU, ID, SO, VO = ("lu", 0, 55), ("id16", 0, 16), ("so", 0, 12), ("vo", 0, 240)
-    li("lu", ("c1", 55), [INP], [LU], T.lu[:, 0:55], T.inp[:])
-    li("k0", ("c1", 8), [INP], [("kl", 0, 8)], T.kl[:, 0:8], T.inp[:, 8:16], 1.0 / 128, -0.5 + 1.0 / 256)
-    li("sf", ("c1", 8), [INP], [("sf", 0, 8)], T.sf[:], T.inp[:, 16:24], 2.0 ** -14, 0.0)
-    li("sod", ("c1", 3), [INP, pcr(0)], [SO], T.so[:, 0:12:4], T.inp[:, 40:55:5], 128.0, col(0))
-    li("vo", ("g", 240), [LU, ID], [VO], T.vo[:], T.id16[:].indirect(T.lu[:, 40:55]))
-    li("qm", ("g", 256), [LU, ID], [("qm", 0, 256)], T.qm[:], T.id16[:].indirect(T.lu[:, 24:40]))
-    for b, a, c in (("rea", 256, 40), ("ry", 256, 45), ("zc", 640, 50)):
-        li("let" + b, ("c1", 5), [INP], [(b, a, a + 5)], T[b][:, a:a + 5], T.inp[:, c:c + 5])
+    lin("lu", v("lu", 0, 55), v("inp"))
+    lin("k0", v("kl", 0, 8), v("inp", 8, 16), 1.0 / 128, -0.5 + 1.0 / 256)
+    lin("sf", v("sf"), v("inp", 16, 24), 2.0 ** -14, 0.0)
+    lin("sod", v("so", 0, 12, 4), v("inp", 40, 55, 5), 128.0, col(0))
+    lin("vo", v("vo"), at(v("id16"), v("lu", 40, 55)))
+    for t in range(2):
+        lin("qm%d" % t, v("qm", 128 * t, 128 * t + 128), at(v("id16"), v("lu", 24 + 8 * t, 32 + 8 * t)))
+    for b, a, c in (("rea", 128, 40), ("ry", 128, 45), ("zr", 128, 50)):
+        lin("let" + b, v(b, a, a + 5), v("inp", c, c + 5))
 
-    def onehots(tag, w, vo, vr, v0, so, s0, sr):
-        k = wid[w] // 2048
-        scat(tag + "a", 16 * k, [sr, vr], "pb%d" % (2 * w), 0, wid[w], so[:, s0:s0 + k], vo[:, v0 + 16:v0 + 16 + 16 * k])
-        if need_d[w]:
-            scat(tag + "b", 32, [SO, vr], "pb%d" % (2 * w + 1), 0, 4096, T.so[:, 2:4], vo[:, v0 + 48:v0 + 80])
-        if need_t[w]:
-            scat(tag + "c", 48, [("st", 0, 4), vr], "sm", 384 * w, 384 * w + 384, T.st[:, 0:3], vo[:, v0 + 32:v0 + 80])
+    def onehots(tag, w, vo, v0, so, s0):
+        scat(tag + "a", pbv(4 * w, 2), v(so, s0, s0 + 2), v(vo, v0 + 16, v0 + 48))
+        scat(tag + "b", pbv(4 * w + 2, 2), v("so", 2, 4), v(vo, v0 + 48, v0 + 80))
 
     for w in range(3):
-        onehots("sp%d" % w, w, T.vo, VO, 80 * w, T.so, 4 * w, SO)
+        onehots("sp%d" % w, w, "vo", 80 * w, "so", 4 * w)
 
     def parts(s):
-        return [(128 * i // split[s], 128 * (i + 1) // split[s]) for i in range(split[s])]
+        n = cfg["cut"][s]
+        return [(128 * i // n, 128 * (i + 1) // n) for i in range(n)]
 
-    def gather(name, s, win, winr, bias):
+    def gather(i, s, win, bias):
         for a, b in parts(s):
-            li("%s_%d" % (name, a), ("g", 16 * (b - a)), [winr, ("o" + s, a, b)], [("g" + s, 16 * a, 16 * b)],
-               T["g" + s][:, 16 * a:16 * b], win.indirect(T["o" + s][:, a:b]), 1.0, bias)
+            lin("g%s%d_%d" % (s, i, a), v("g" + s, 16 * a, 16 * b), at(v(win), v("o" + s, a, b)), 1.0, bias)
 
     def pick(i, s, src, w, dst, d0, bias):
-        gs = T["g" + src]
+        base = 2048 * (4 * w + i - 1)
         for a, b in parts(s):
-            tile, n = "%s%d_%d" % (s, i, a), b - a
-            gr = ("g" + src, 16 * a, 16 * b)
-            if i > 1 and s in turn:
-                m0 = 384 * w + 128 * (i - 2)
-                pe("t" + tile, 1024, [gr, ("sm", m0, m0 + 128)],
-                   lambda ps, a=a, b=b: [(ps[0:b - a, j:128:16], gs[:, 16 * a + j:16 * b:16], T.sm[:, m0 + 8 * j:m0 + 8 * j + 8], True, True) for j in range(16)])
-                tm = T["u" + s]
-                lp("d" + tile, "t" + tile, 0, 128, [], [("u" + s, 0, 128)], tm[0:n, :], p=n)
-                pe(tile, max(64, n), [("u" + s, 0, 128), ("idb", 0, 128)], lambda ps, n=n: [(ps[:, 0:n], tm[0:n, :], T.idb[0:n, 0:n], True, True)])
-            else:
-                pb, base = "pb%d" % (2 * w + (i - 1) // 2), 2048 * ((i - 1) % 2)
-                pe(tile, 16 * max(64, n), [gr, (pb, base, base + 2048)],
-                   lambda ps, a=a, b=b, pb=pb, base=base: [(ps[:, 0:b - a], T[pb][:, base + 128 * j:base + 128 * j + 128],
-                                                            gs[:, 16 * a + j:16 * b:16], j == 0, j == 15) for j in range(16)])
-            lp("c" + tile, tile, 0, n, [], [(dst, d0 + a, d0 + b)], T[dst][:, d0 + a:d0 + b], 1.0, bias)
-            if i == 4 and s in ("Yq", "Zr"):
-                u = 128 * (s == "Zr")
-                lp("e" + tile, tile, 0, n, [], [("dup", u + a, u + b)], T.dup[:, u + a:u + b])
+            tile = "%s%d_%d" % (s, i, a)
+            pe("p" + tile, acc(ps(tile, 0, b - a), [(v("pb", base + 128 * j, base + 128 * j + 128), v("g" + src, 16 * a + j, 16 * b, 16))
+                                                    for j in range(16)]))
+            if i == 4 and s == "Zr":
+                tt("dif1_%d" % a, v("df", 136 + a, 136 + b), ps(tile, 0, b - a), v("zm", a, b), AL.not_equal)
+            lin("c" + tile, v(dst, d0 + a, d0 + b), ps(tile, 0, b - a), 1.0, bias)
 
-    def walk(s, src, w, dst, d0):
-        pick(1, s, src, w, "o" + s, 0, HALF)
-        gather("g" + s + "2", s, T.xi[:], XI, -HALF)
-        pick(2, s, s, w, "o" + s, 0, HALF)
-        gather("g" + s + "3", s, T.xi[:], XI, -HALF)
-        pick(3, s, s, w, "o" + s, 0, HALF)
-        gather("g" + s + "4", s, T.oi[:], OI, 0.0)
-        pick(4, s, s, w, dst, d0, 0.0)
+    def walk(s, w, dst, d0, upto=5):
+        pick(1, s, s[1], w, "o" + s, 0, HALF)
+        for i in (2, 3):
+            gather(i, s, "xi", -HALF)
+            pick(i, s, s, w, "o" + s, 0, HALF)
+        gather(4, s, "oi", 0.0)
+        if upto > 4:
+            pick(4, s, s, w, dst, d0, 0.0)
 
-    def queries(t, s, width):
-        a, kl, ql = 128 * t, T.kl[:, 8 * t:8 * t + 8], T.ql[:, 8 * t:8 * t + 8]
-        tr, qr = ("t16", a, a + 128), ("ql", 8 * t, 8 * t + 8)
-        op("qc%d" % t, "V", ("g", 128), [("nxc", 0, width), ("kl", 8 * t, 8 * t + 8), ("qm", 0, 256)], [tr],
-           lambda e, ps: V.tensor_tensor(T.t16[:, a:a + 128], T.nxc[:, 0:width].indirect(kl), T.qm[:, a:a + 128], AL.mult))
-        pe("q%d" % t, 1024, [tr, ("w2", 0, 144)],
-           lambda ps: [(ps[:, 0:8], T.w2[:, 15 - r:143 - r], T.t16[:, a + r:a + 128:16], r == 0, r == 15) for r in range(16)])
-        lp("cq%d" % t, "q%d" % t, 0, 8, [], [qr], ql, 1.0, HALF)
-        li("s0" + s, ("g", 128), [XI, qr], [("o" + s, 0, 128)], T["o" + s][:], T.xi[:].indirect(ql))
-        gather("g" + s + "1", s, T.xi[:], XI, -HALF)
+    def slide(tile, a, b, buf, c0, rhs, more=()):
+        return acc(ps(tile, a, b), [(v(buf, c0 + 15 - r, c0 + 143 - r), rhs(r)) for r in range(16)] + list(more))
 
-    def match(t, qb, q0, rb, kc):
-        a = 128 * t
-        qr, qa = (qb, q0, q0 + 128), T[qb][:, q0:q0 + 128]
+    def queries(t, s):
+        a, ql = 128 * t, v("ql", 8 * t, 8 * t + 8)
+        tt("qc%d" % t, v("t16", a, a + 128), at(v("nxc", 0, 128 + a), v("kl", 8 * t, 8 * t + 8)), v("qm", a, a + 128), AL.mult)
+        pe("pq%d" % t, slide("q%d" % t, 0, 8, "w2", 0, lambda r: v("t16", a + r, a + 128, 16)))
+        lin("cq%d" % t, ql, ps("q%d" % t, 0, 8), 1.0, HALF)
+        lin("s0" + s, v("o" + s), at(v("xi"), ql))
+        gather(1, s, "xi", -HALF)
+
+    def row(a, b):
+        return v("blk"), v("cst", a, b)
+
+    def match(t, qb, rb, r0):
+        a, kc, m0, n0 = 128 * t, 128 + 128 * t, 256 * t, 144 * t
+        q, r = v(qb, 0, 128), v(rb, r0, r0 + kc)
         for h in range(2):
-            o = 256 * t + 128 * h
-            li("qh%d%d" % (t, h), ("ch", 128), [qr, pcr(7 + h)], [("qh", o, o + 128)], T.qh[:, o:o + 128], qa, col(7 + h), 0.0)
-        op("q2%d" % t, "A", ("c1", 128), [qr], [("q2", a, a + 128)], lambda e, ps: g.scalar.activation(T.q2[:, a:a + 128], qa, AF.Square))
-        op("r2%d" % t, "A", ("c1", kc), [(rb, 0, kc)], [("r2", a, a + kc)],
-           lambda e, ps: g.scalar.activation(T.r2[:, a:a + kc], T[rb][:, 0:kc], AF.Square))
+            lin("rm%d%d" % (t, h), v("rm", m0 + kc * h, m0 + kc * h + kc), r, col(7 + h), 0.0)
+        op("r2%d" % t, "A", [("square", (v("r2", a, a + kc), r))])
+        op("q2%d" % t, "A", [("square", (v("q2", a, a + 128), q))])
         for b in range(4):
-            tile = "m%d%d" % (t, b)
-
-            def seq(ps, p=slice(32 * b, 32 * b + 32)):
-                s = []
-                for h in range(2):
-                    out, eh = ps[:, kc * h:kc * h + kc], T.ee[p, 128 * h:128 * h + 128]
-                    s += [(out, eh, T.kv[p, 0:kc], True, False), (out, eh, T.r2[p, a:a + kc], False, False),
-                          (out, T.qh[p, 256 * t + 128 * h:256 * t + 128 * h + 128], T[rb][p, 0:kc], False, True)]
-                return s
-            pe(tile, 6 * kc, [("ee", 0, 256), ("kv", 0, 256), ("r2", a, a + kc), ("qh", 256 * t, 256 * t + 256), (rb, 0, kc)], seq)
+            tile, p = "m%d%d" % (t, b), (32 * b, 32 * b + 32)
+            pe("a" + tile, [(ps(tile, 0, 2 * kc), v("one", p=(p[0], p[0] + 1)), v("kv", m0, m0 + 2 * kc, p=(p[0], p[0] + 1)), True, True)]
+               + [(ps(tile, kc * h, kc * h + kc), v("ee", 128 * h, 128 * h + 128, p=p), v("r2", a, a + kc, p=p), False, True) for h in range(2)],
+               last=False)
+            pe("b" + tile, [(ps(tile, 0, 2 * kc), v(qb, 0, 128, p=p), v("rm", m0, m0 + 2 * kc, p=p), False, True)])
             for h in range(2):
                 j = 8 * t + 2 * b + h
-                op("rd%d" % j, "V", ("c1", kc), [], [("mn", j, j + 1)],
-                   lambda e, ps, j=j, h=h: V.tensor_reduce(T.mn[:, j:j + 1], ps[:, kc * h:kc * h + kc], AxisListType.X, AL.min), pr=tile)
-        tile = "k%d" % t
-        pe(tile, 640, [("mn", 8 * t, 8 * t + 8), ("idf", 0, 128), ("indk", 0, 8), ("q2", a, a + 128)],
-           lambda ps: [(ps[0:8, 0:128], T.indk[:], T.q2[:, a:a + 128], True, False),
-                       (ps[0:8, 0:128], T.mn[:, 8 * t:8 * t + 8], T.idf[:], False, True)])
-        nh, cum, tt = T.nh[0:8, a:a + 128], T.cum[0:8, a:a + 128], T.tt[0:8, a:a + 128]
-        nr, cr, tr, ones = ("nh", a, a + 128), ("cum", a, a + 128), ("tt", a, a + 128), ("rows", 256, 384)
-        op("nh%d" % t, "V", ("c1", 128), [], [nr], lambda e, ps: V.tensor_scalar(nh, ps[0:8, 0:128], 1024.0, -1.0, AL.is_lt, AL.mult), pr=tile)
-        own = T.ic[0:8, 128:256] if t == 0 else T.rows[0:8, 0:128]
-        l0 = 256 * t
-        op("cmp%d" % t, "V", ("c1", 128), [icr, ("rows", 0, 128)], [("ls", l0, l0 + 128)],
-           lambda e, ps: V.tensor_tensor(T.ls[0:8, l0:l0 + 128], ps[0:8, 0:128], own, AL.min), pr=tile)
-        init = 127.0 if t == 0 else T.cum[0:8, 127:128]
-        op("cum%d" % t, "V", ("c1", 128), [nr, ones, ("cum", 0, a)], [cr],
-           lambda e, ps: V.tensor_tensor_scan(cum, nh, T.rows[0:8, 256:384], init, AL.add, AL.add))
-        op("tt%d" % t, "V", ("c2", 128), [nr, ("rows", 128, 256)], [tr], lambda e, ps: V.tensor_tensor(tt, nh, T.rows[0:8, 128:256], AL.mult))
-        op("scl%d" % t, "V", ("c2", 128), [cr, tr], [("ls", l0 + 128, l0 + 256)],
-           lambda e, ps: V.tensor_tensor(T.ls[0:8, l0 + 128:l0 + 256], cum, tt, AL.max))
-        op("ym%d" % t, "V", ("c1", 128), [cr], [("yms", a, a + 128)],
-           lambda e, ps: V.tensor_tensor(T.yms[0:8, a:a + 128], ps[0:8, 0:128], cum, AL.min), pr=tile)
+                red("rd%d" % j, v("mn", j, j + 1), ps(tile, kc * h, kc * h + kc), AL.min)
+        mn, md, new = v("mn", 8 * t, 8 * t + 8), v("md", 8 * t, 8 * t + 8), v("nw", n0 + 15, n0 + 143, 16)
+        th, l, k, cu = ("%s%d" % (x, t) for x in ("th", "l", "hit", "cu"))
+        pe("p" + th, acc(ps(th, 0, 8), [row(16, 24), (v("q2", a, a + 128), v("indk"))]))
+        tt("new%d" % t, new, mn, ps(th, 0, 8), AL.is_ge)
+        tt("md%d" % t, md, mn, ps(th, 0, 8), AL.subtract)
+        n = 9 - t
+        pe("p" + l, slide(l, 0, n, "nw", n0, lambda r: v("mx", r, 16 * n, 16), [row(0, n)]))
+        lin("c" + l, v("ll", 16 * t, 16 * t + 8), ps(l, 0, 8), 1.0, col(4 + 10 * t))
+        ts("ms%d" % t, v("ms", n0 + 15, n0 + 143, 16), md, 256.0, float(kc), AL.add, AL.min)
+        pe("p" + k, slide(k, 0, 8, "ms", n0, lambda r: v("idb", r, 128, 16)))
+        lin("c" + k, v("ll", 16 * t + 8, 16 * t + 16), ps(k, 0, 8))
+        pe("p" + cu, acc(ps(cu, 0, 8), [row(24, 32), (v("tri"), new)] + [(v("one"), v("nw", 15, 143, 16))] * t))
+        tt("ym%d" % t, v("rc", R0 + 384 + 8 * t, R0 + 392 + 8 * t), md, ps(cu, 0, 8), AL.min)
 
-        def lists(ps):
-            s = [(ps[:, 0:16], T.w1[0:8, 15 - r:143 - r], T.ls[0:8, l0 + r:l0 + 256:16], r == 0, r == 15) for r in range(16)]
-            if t == 0:
-                s += [(ps[:, 16:17], T.ind8[0:8, :], T.cum[0:8, 127:128], True, False),
-                      (ps[:, 16:17], T.ind8[0:8, :], T.rows[0:8, 256:257], False, True)]
-            return s
-        pe("l%d" % t, 1536 - 512 * t, [("w1", 0, 144), ("ls", l0, l0 + 256), ("ind8", 0, 128), cr, ones], lists)
-        lp("cl%d" % t, "l%d" % t, 0, 16, [], [("ll", 16 * t, 16 * t + 16)], T.ll[:, 16 * t:16 * t + 16])
-
-    def winner(t, wb, wn):
-        d0, w0, sd = 136 * t, 144 * t, T.sd[:, 16 * t:16 * t + 16]
-        op("dif%d" % t, "V", ("g", 128), [(wb, 0, wn), ("dup", 128 * t, 128 * t + 128), ("ll", 16 * t, 16 * t + 16)], [("df", d0, d0 + 128)],
-           lambda e, ps: V.tensor_tensor(T.df[:, d0:d0 + 128], T[wb][:, 0:wn].indirect(T.ll[:, 16 * t:16 * t + 8]),
-                                         T.dup[:, 128 * t:128 * t + 128], AL.not_equal))
-        sc, gm = T.sc[:, 2 * t:2 * t + 1], T.sc[:, 2 * t + 1:2 * t + 2]
-        sr, dr = ("sc", 2 * t, 2 * t + 1), ("sd", 16 * t, 16 * t + 16)
-        op("sco%d" % t, "V", ("c1", 129), [("df", d0, d0 + 129)], [sr], lambda e, ps: V.tensor_reduce(sc, T.df[:, d0:d0 + 129], AxisListType.X, AL.add))
-        li("sd%d" % t, ("c1", 16), [sr, ID], [dr], sd, T.id16[:], sc, 0.0)
-        pe("w%d" % t, 256, [("blk", 0, 128), dr], lambda ps: [(ps[:, 0:16], T.blk[:], sd, True, True)])
-        op("gm%d" % t, "V", ("c1", 16), [], [("sc", 2 * t + 1, 2 * t + 2)],
-           lambda e, ps: V.tensor_reduce(gm, ps[:, 0:16], AxisListType.X, AL.max), pr="w%d" % t)
+    def winner(t):
+        d0, w0, sd, tile = 136 * t, 144 * t, v("sd", 16 * t, 16 * t + 16), "w%d" % t
+        sc, gm = v("sc", 2 * t, 2 * t + 1), v("sc", 2 * t + 1, 2 * t + 2)
+        red("sco%d" % t, sc, v("df", d0, d0 + 130), AL.add)
+        lin("sd%d" % t, sd, v("id16"), sc, 0.0)
+        pe("p" + tile, acc(ps(tile, 0, 16), [(v("blk"), sd)]))
+        red("gm%d" % t, gm, ps(tile, 0, 16), AL.max)
         a, b = (15, 143) if t == 0 else (0, 144)
-        ts("ww%d" % t, ("ch", b - a), [("w2", 0, 144), ("sc", 2 * t, 2 * t + 2)], [("ww", w0, w0 + 144)],
-           T.ww[:, w0 + a:w0 + b], T.w2[:, a:b], gm, sc, AL.mult, AL.is_equal)
+        ts("ww%d" % t, v("ww", w0 + a, w0 + b), v("wa", a, b), gm, sc, AL.add, AL.is_equal)
 
-    li("s0b", ("g", 128), [TB, LU], [("ob", 0, 128)], T.ob[:], T.tb[:].indirect(T.lu[:, 0:8]), 1.0 / 16, RND)
-    li("nxb", ("g", 128), [TB, LU], [("nxc", 0, 128)], T.nxc[:, 0:128], T.tb[:].indirect(T.lu[:, 0:8]), 1.0 / 16, RND - HALF)
-    gather("gb1", "b", T.xi[:], XI, -HALF)
-    queries(0, "q", 128)
-    li("nxq", ("c1", 128), [("oq", 0, 128)], [("nxq", 0, 128)], T.nxq[:], T.oq[:], 1.0, -HALF)
-    walk("Eb", "b", 0, "rea", 0)
-    walk("Eq", "q", 0, "rea", 128)
-    walk("Yb", "b", 1, "ry", 0)
-    walk("Yq", "q", 1, "ry", 128)
-    walk("Zb", "b", 2, "zc", 0)
-    walk("Zq", "q", 2, "zq", 0)
-    scat("clr", 16, [SO, ("zsrc", 0, 1024)], "pb0", 0, 2048, T.so[:, 0:1], T.zsrc[:, 0:16])
-    match(0, "rea", 128, "rea", 128)
-    op("k1", "V", ("c1", 8), [("sf", 0, 8)], [("kl", 8, 16)],
-       lambda e, ps: V.tensor_scalar(T.kl[:, 8:16], T.sf[:], ps[:, 16:17], -0.5 + 2.0 ** -15, AL.mult, AL.add), pr="l0")
-    L0, L1 = ("ll", 0, 16), ("ll", 16, 32)
-    scat("snx", 128, [L0, ("nxq", 0, 128)], "nxc", 0, 512, T.ll[:, 8:16], T.nxq[:])
-    queries(1, "r", 256)
-    scat("szq", 128, [L0, ("zq", 0, 128)], "zc", 0, 512, T.ll[:, 8:16], T.zq[:])
-    winner(0, "ry", 256)
-    pe("u", 522, [("keep0", 0, 128), ("rea", 0, 261), ("ww", 0, 144), ("ry", 0, 261)],
-       lambda ps: [(ps[:, 0:261], T.keep0[:], T.rea[:, 0:261], True, False), (ps[:, 0:261], T.ww[:, 15:143], T.ry[:, 0:261], False, True)])
-    lp("elu", "u", 256, 261, [], [("elu", 0, 6)], T.elu[:, 0:5])
-    lp("so2", "u", 256, 257, [pcr(0)], [("so2", 0, 1)], T.so2[:, 0:1], 128.0, col(0))
-    lp("urc", "u", 0, 128, [], [("rc", 0, 128)], T.rc[:, 0:128])
-    lp("urt", "u", 128, 261, [], [("rt", 0, 136)], T.rt[:, 0:133])
-    li("vo2", ("g", 80), [("elu", 0, 6), ID], [("vo2", 0, 80)], T.vo2[:], T.id16[:].indirect(T.elu[:, 0:5]))
-    onehots("sq", 0, T.vo2, ("vo2", 0, 80), 0, T.so2, 0, ("so2", 0, 2))
-    scat("srt", 128, [L0, ("rt", 0, 136)], "rc", 0, 512, T.ll[:, 8:16], T.rt[:, 0:128])
+    lin("s0b", v("ob"), at(v("tb"), v("lu", 0, 8)), 1.0 / 16, RND)
+    lin("nxb", v("nxc", 0, 128), at(v("tb"), v("lu", 0, 8)), 1.0 / 16, RND - HALF)
+    gather(1, "b", "xi", -HALF)
+    queries(0, "q")
+    lin("nxq", v("nxq"), v("oq"), 1.0, -HALF)
+    walk("Eb", 0, "rea", 144)
+    walk("Eq", 0, "rea", 0)
+    walk("Yb", 1, "ry", 144)
+    walk("Yq", 1, "ry", 0)
+    walk("Zb", 2, "zc", 0)
+    walk("Zq", 2, "zq", 0)
+    scat("clr", pbv(0), v("so", 0, 1), v("zsrc", 0, 16))
+    match(0, "rea", "rea", 144)
+    ts("k1", v("kl", 8, 16), v("sf"), ps("l0", 8, 9), -0.5 + 2.0 ** -15, AL.mult, AL.add)
+    lin("pc14", col(14), ps("l0", 8, 9), 1.0, col(4))
+    lin("pc14b", col(14), col(14), 1.0, -128.0)
+    L0, L1 = v("ll", 0, 8), v("ll", 16, 24)
+    scat("snx", v("nxc"), L0, v("nxq"))
+    queries(1, "r")
+    scat("szq", v("zc"), L0, v("zq"))
+    tt("dif0", v("df", 0, 128), at(v("ry", 144, 288), v("ll", 8, 16)), v("ry", 0, 128), AL.not_equal)
+    winner(0)
+    pe("pu", acc(ps("u", 0, 272), [(v("keep0"), v("rea")), (v("ww", 15, 143), v("ry", 0, 272))]))
+    lin("elu", v("elu", 0, 5), ps("u", 128, 133))
+    lin("so2", v("so2", 0, 1), ps("u", 128, 129), 128.0, col(0))
+    lin("urc", v("rc", 0, 272), ps("u", 0, 272))
+    lin("vo2", v("vo2"), at(v("id16"), v("elu", 0, 5)))
+    onehots("sq", 0, "vo2", 0, "so2", 0)
+    scat("srt", v("rc", R0), L0, v("rc", 0, 128))
 
-    walk("Er", "r", 0, "rq", 0)
-    walk("Zr", "r", 2, "zc", 512)
-    match(1, "rq", 0, "rc", 256)
-    dma("ymd", "S", 2.0, [("yms", 0, 256)], [("yd", 0, 1)], [(T.yd[:], T.yms[0:8, :])], "ymd")
-    scat("srq", 128, [L1, ("rq", 0, 128)], "rc", 0, 512, T.ll[:, 24:32], T.rq[:])
-    send("rc", 0.5, 3.5, ("rc", 0, 384), ("rcl", 0, 384), T.rcl[:], T.rc[:, 0:384])
-    send("ym", 0.5, 2.0, ("yd", 0, 1), ("yl", 0, 1), T.yl[:], T.yd[:])
-    li("rcf", ("ch", 384), [("rcl", 0, 384)], [("rcf", 0, 384)], T.rcf[:], T.rcl[:])
-    dma("oyr", "S", 2.6, [("rcf", 0, 384)], [("yr", 0, 1)], [(T.yr[:], T.rcf[:])], "oyr")
-    dma("oym", "S", 2.0, [("yl", 0, 1)], [("ym", 0, 1)], [(T.ym[:], T.yl[:])], "oym")
-    winner(1, "zc", 640)
-    scat("szr", 128, [L1, ("zc", 512, 640)], "zc", 0, 512, T.ll[:, 24:32], T.zc[:, 512:640])
-    pe("f", 1152, [("ww", 144, 288), ("zc", 0, 645), ("keep1", 0, 128), ("rt", 0, 136)],
-       lambda ps: [(ps[:, 0:24], T.ww[:, 159 - r:287 - r], T.zc[:, 24 * r:24 * r + 24], r == 0, r == 15) for r in range(16)]
-       + [(ps[:, 24:29], T.keep1[:], T.rt[:, 128:133], True, False), (ps[:, 24:29], T.ww[:, 158:286], T.zc[:, 640:645], False, True)])
-    lp("fin", "f", 0, 29, [], [("fin", 0, 29)], T.fin[:])
-    send("fin", 0.5, 2.5, ("fin", 0, 29), ("finl", 0, 29), T.finl[:], T.fin[:])
-    dma("ofin", "S", 2.0, [("finl", 0, 29)], [("yr", 0, 1)], [(T.yr[1::16, :], T.finl[:, 0:24])], "ofin")
-    dma("oye", "A", 2.0, [("finl", 0, 29)], [("ye", 0, 1)], [(T.ye[:], T.finl[:, 24:29])], "ofin")
+    walk("Er", 0, "rq", 0)
+    walk("Zr", 2, "zr", 0, 4)
+    match(1, "rq", "rc", R0)
+    scat("srq", v("rc", R0), L1, v("rq"))
+    send("rc", 2.0, 1.0, v("rcl"), v("rc", R0, R0 + 400))
+    lin("rcf", v("rcf"), v("rcl", 0, 384))
+    runs = [(max(16 * k - 14, 0), min(16 * k + 1, 128)) for k in range(9)]
+    dma("oyr", "S", 2.0, [(("d", "yr", 0, 1, (slice(a, b), ALL)), v("rcf", p=(a, b))) for a, b in runs])
+    pe("py", [(ps("y", 128 * t, 128 * t + 128, (0, 8)), v("rcl", 384 + 8 * t, 392 + 8 * t), v("idb"), True, True) for t in range(2)])
+    lin("ymf", v("ymf", p=(0, 8)), ps("y", 0, 256, (0, 8)), 1.0, 256.0)
+    dma("oym", "A", 1.6, [(hbm("ym", ALL), v("ymf", p=(0, 8)))])
+    lin("zm", v("zm"), at(v("zc", 0, 272), v("ll", 24, 32)))
+    pick(4, "Zr", "Zr", 2, "zr", 0, 0.0)
+    winner(1)
+    scat("szr", v("zc"), L1, v("zr", 0, 128))
+    pe("pf", slide("f", 0, 24, "ww", 144, lambda r: v("zc", 24 * r, 24 * r + 24))
+       + acc(ps("f", 24, 29), [(v("keep1"), v("rc", 128, 133)), (v("ww", 158, 286), v("zr", 128, 133))]))
+    lin("fin", v("fin"), ps("f", 0, 29))
+    send("fin", 1.0, 1.0, v("finl"), v("fin"))
+    dma("ofin", "S", 1.6, [(("d", "yr", 1, 2, (slice(1, None, 16), ALL)), v("finl", 0, 24))])
+    dma("oye", "A", 1.6, [(hbm("ye", ALL), v("finl", 24, 29))])
     return ops
 
 
 def data_deps(ops):
-    by, tiles, deps = {}, {}, {}
+    by, deps = {}, {}
     for o in ops:
         acc = [("r",) + x for x in o["r"]] + [("w",) + x for x in o["w"]]
-        d = set(n2 for kind, b, lo, hi in acc for k2, l2, h2, n2 in by.get(b, []) if "w" in (kind, k2) and lo < h2 and l2 < hi)
-        for kind, b, lo, hi in acc:
-            by.setdefault(b, []).append((kind, lo, hi, o["n"]))
-        if o["pw"]:
-            tiles[o["pw"]] = o["n"]
-        if o["pr"]:
-            d.add(tiles[o["pr"]])
-        deps[o["n"]] = d
+        deps[o["n"]] = set(n2 for kind, m, b, lo, hi in acc for k2, l2, h2, n2 in by.get((m, b), [])
+                           if "w" in (kind, k2) and (m == "p" or (lo < h2 and l2 < hi)))
+        for kind, m, b, lo, hi in acc:
+            by.setdefault((m, b), []).append((kind, lo, hi, o["n"]))
+        o["pw"] = ([b for m, b, lo, hi in o["w"] if m == "p"] + [None])[0]
+        o["pr"] = ([b for m, b, lo, hi in o["r"] if m == "p"] + [None])[0]
     return deps
 
 
-def parse(text, ops):
-    v = [int(text[i:i + 2], 36) for i in range(0, len(text), 2)]
-    assert sorted(x // 2 for x in v) == list(range(len(ops)))
-    return [(ops[x // 2], ops[x // 2]["e"][x % 2]) for x in v]
-
-
-def emit(g, T, ops, order):
+def emit(g, T, peer, ops, deps, order):
     Q = {"V": g.vector, "A": g.scalar, "P": g.tensor, "G": g, "S": g.sync}
-    deps = data_deps(ops)
+    rid, pid, mask, nen = peer
     left = {}
     for o in ops:
         left[o["pr"]] = left.get(o["pr"], 0) + 1
     free, bank_of, users = list(range(NB)), {}, {}
     chan, seq, know, done, plan, needed = {}, {}, {k: {} for k in Q}, {}, [], set()
     for o, e in order:
-        n, b = o["n"], None
-        d = set(deps[n])
+        n, d = o["n"], set(deps[o["n"]])
         if o["pw"]:
-            b = bank_of[o["pw"]] = free.pop(0)
-            d |= set(users.get(b, []))
-            users[b] = []
+            d = set(x for x in d if chan[x][0] != "cP")
+            if o["pw"] not in bank_of:
+                b = bank_of[o["pw"]] = free.pop(0)
+                d |= set(users.get(b, []))
+                users[b] = []
         if o["pr"]:
             b = bank_of[o["pr"]]
             d |= set(u for u in users[b] if chan[u][0] != "c" + e)
@@ -410,7 +388,7 @@ def emit(g, T, ops, order):
             if left[o["pr"]] == 0:
                 free.append(b)
         seq[e] = seq.get(e, 0) + 1
-        chan[n] = (o["sem"][0], 1) if o["sem"] else ("c" + e, seq[e])
+        chan[n] = (o["sem"], 1) if o["sem"] else ("c" + e, seq[e])
         waits, done[n] = [], {}
         if e != "X":
             k = know[e]
@@ -422,29 +400,55 @@ def emit(g, T, ops, order):
                         k[c2] = max(k.get(c2, 0), v2)
             done[n] = dict(k)
         done[n][chan[n][0]] = chan[n][1]
-        plan.append((o, e, b, waits))
-    count, val, total, waited = {}, {}, {}, set()
-    for o, e, b, waits in plan:
+        plan.append((o, e, waits))
+    count, val, waited = {}, {}, set()
+    for o, e, waits in plan:
         if o["sem"]:
-            total[o["sem"][0]] = total.get(o["sem"][0], 0) + o["sem"][1]
-            val[o["n"]] = o["sem"][1]
+            val[o["n"]] = nen if e in "GX" else 16 * len(o["calls"])
         elif o["n"] in needed:
             count[e] = val[o["n"]] = count.get(e, 0) + 1
-    for o, e, b, waits in plan:
-        if e == "X":
-            continue
+
+    def ap(x):
+        if not isinstance(x, tuple):
+            return x
+        if x[0] == "i":
+            return ap(x[1]).indirect(ap(x[2]))
+        if x[0] == "d":
+            return T[x[1]][x[4]]
+        if x[0] == "x":
+            return ap(x[4])
+        return T[x[1] if x[0] == "s" else "ps%d" % bank_of[x[1]]][x[5][0]:x[5][1], x[2]:x[3]:x[4]]
+
+    def call(e, m, a, sem, small):
+        V = g.vector
+        if m == "lin" and e == "V":
+            return V.tensor_scalar(a[0], a[1], a[2], a[3], AL.mult, AL.add)
+        if m == "lin":
+            return g.scalar.activation(a[0], a[1], AF.Copy if isinstance(a[3], float) else AF.Identity, bias=a[3], scale=a[2])
+        if m == "square":
+            return g.scalar.activation(a[0], a[1], AF.Square)
+        if m == "iota":
+            return g.iota(*a, allow_small_or_imprecise_dtypes=True) if small else g.iota(*a)
+        if m == "remote_dma":
+            return g.remote_dma(a[0], a[1], T.sem["a" + sem[1:]], T.sem[sem], pid, rid, mask)
+        if m == "dma_start":
+            return Q[e].dma_start(*a).then_inc(T.sem[sem], 16)
+        if m == "matmul":
+            return g.tensor.matmul(*a)
+        return {"memset": V.memset, "tensor_copy": V.tensor_copy, "tensor_scalar": V.tensor_scalar, "tensor_tensor": V.tensor_tensor,
+                "tensor_reduce": V.tensor_reduce}[m](*a)
+
+    for o, e, waits in plan:
         for x in waits:
             Q[e].wait_ge(T.sem[chan[x][0]], val[x])
-            waited.add(chan[x][0])
-        ins = o["f"](e, None if b is None else T["ps%d" % b])
-        if o["sem"]:
-            for i in (ins if e != "G" else []):
-                i.then_inc(T.sem[o["sem"][0]], 16)
-        elif o["n"] in needed:
+            waited.add(x)
+        for m, a in o["calls"]:
+            ins = call(e, m, [ap(x) for x in a], o["sem"], m == "iota" and SB[a[0][1]][1] != I32)
+        if o["n"] in needed and not o["sem"]:
             ins.then_inc(T.sem["c" + e], 1)
-    for s, v in total.items():
-        if s not in waited:
-            Q["G" if s == "lsem" else "S"].wait_ge(T.sem[s], v)
+    for o, e, waits in plan:
+        if o["sem"] and o["n"] not in waited:
+            Q["G" if e == "G" else "S"].wait_ge(T.sem[o["sem"]], val[o["n"]])
 
 
 def rank_program(g, core, T, topo):
@@ -454,5 +458,83 @@ def rank_program(g, core, T, topo):
     n = len(T.cores)
     other = T.cores[(rank + n // 2) % n]
     rid, pid = topo.addr(other, core)
-    ops = make_ops(g, T, (rid, pid, topo.mask(core, other), len(topo.engines(core, other))), CFG)
-    emit(g, T, ops, parse(ORDER, ops))
+    ops = make_ops(CFG)
+    deps = data_deps(ops)
+    emit(g, T, (rid, pid, topo.mask(core, other), len(topo.engines(core, other))), ops, deps, parse(ops) if CFG.get("order") else deal(ops, deps, CFG))
+
+
+def parse(ops):
+    t = CFG["order"]
+    return [(ops[x // 2], ops[x // 2]["e"][x % 2]) for x in (int(t[i:i + 2], 36) for i in range(0, len(t), 2))]
+
+
+def deal(ops, deps, cfg):
+    hop, by = cfg["hop"], {o["n"]: o for o in ops}
+    num = {o["n"]: i for i, o in enumerate(ops)}
+    succ = {o["n"]: [] for o in ops}
+    for n, d in deps.items():
+        for x in d:
+            succ[x].append(n)
+    jobs = {}
+    for o in ops:
+        jobs.setdefault(o["pw"] or o["pr"] or o["n"], []).append(o["n"])
+    job = {n: j for j, m in jobs.items() for n in m}
+    need = {j: set(job[x] for n in m for x in deps[n]) - {j} for j, m in jobs.items()}
+    for e in "GS":
+        line = [o["n"] for o in ops if o["e"] == e]
+        for a, b in zip(line, line[1:]):
+            need[b].add(a)
+    lets = {j: [k for k in jobs if j in need[k]] for j in jobs}
+
+    def lag(x, y):
+        return by[x]["late"] + (0.0 if by[x]["e"] == by[y]["e"] == "P" else hop)
+
+    def gap(line, t, c):
+        for a, b in line:
+            if t + c <= a + 1e-9:
+                break
+            t = max(t, b)
+        return t
+
+    way = {}
+    for o in reversed(ops):
+        way[o["n"]] = min([-o["late"]] + [way[x] - lag(o["n"], x) for x in succ[o["n"]]]) - min(o["c"].values())
+    urge = {n: w - sum(x for k, x in cfg["lead"].items() if k in n) for n, w in way.items()}
+    busy, when, life = {e: [] for e in "VAPGSX"}, {}, []
+    left = {j: len(d) for j, d in need.items()}
+    free = [j for j in jobs if not left[j]]
+
+    def place(m, t0):
+        prev = None
+        for n in m:
+            o, opts = by[n], []
+            t = max([t0] + [when[y][1] + lag(y, n) for y in deps[n]] + [b for a, b in busy[o["e"][0]][-1:] if o["e"] in "GS"])
+            for e in o["e"]:
+                s = gap(busy[e], max(t, when[prev][1] + hop) if o["pr"] and when[prev][2] != e else t, o["c"][e])
+                opts.append((s + o["c"][e] + cfg["lean"] * ((e == "A") == (o["c"][e] < 0.5)), s, e))
+            f, s, e = min(opts)
+            busy[e].append((s, s + o["c"][e]))
+            busy[e].sort()
+            when[n], prev = (s, s + o["c"][e], e), n
+
+    while free:
+        j = min(free, key=lambda k: (min(urge[n] for n in jobs[k]), num[jobs[k][0]]))
+        free.remove(j)
+        m, t0 = jobs[j], 0.0
+        if by[m[0]]["pw"] and by[m[1]]["pw"]:
+            t0 = max(when[y][1] for y in deps[m[1]] if y not in m) - cfg["early"]
+        place(m, t0)
+        while by[m[0]]["pw"]:
+            a, b = when[m[0]][0], max(when[n][1] for n in m) + hop
+            over = [(x, y) for x, y in life if x < b and a < y]
+            if all(sum(1 for x, y in over if x <= p < y) < NB for p in [a] + [x for x, y in over if x > a]):
+                life.append((a, b))
+                break
+            for n in m:
+                busy[when[n][2]].remove(when[n][:2])
+            place(m, min(y for x, y in over if y > a))
+        for k in lets[j]:
+            left[k] -= 1
+            if not left[k]:
+                free.append(k)
+    return [(by[n], when[n][2]) for n in sorted(when, key=lambda n: (when[n][0], num[n]))]

from concourse.mybir import AluOpType, AxisListType, ActivationFunctionType

AL = AluOpType
AF = ActivationFunctionType
C = 3072
HALF = 1536.0
RND = -0.46875
CFG = {"chunks": [0, 1024, 2048, 2688, 3072],
       "cut": {"b": 2, "q": 2, "r": 2, "Eb": 2, "Eq": 2, "Er": 2, "Yb": 2, "Yq": 2, "Zb": 2, "Zq": 2, "Zr": 2},
       "order": "000c0o020e0406080a0g0i24260s280q0k2a3g2s102e2q2k2w3q2m3i2h2j2o3n3a2d3c3l2v2y3t3p383e3v3w303632343z401243440m0u47480w0y1416181a1c1e1g1i1k1m1o1q1s1u1w1y20224b4h4d57595b4q4k4i5e5g5c5j4n4u5w5l5n5s5z5o5v704w634y9g7473604o889j796876647a7c9o7g667e7i6b8b6f8c8h8e9k9s8k6k6c9n6g507l7m7o8j9u527r6i7s7v7x7z5rao8obw8m6m6o6s6qby6w80846u8sa16y82da87d68wd9du9qdc8rdedw4edmdodg8ya4are0dqe2eadke48vdydia7e8959w90dse69yeca2egeu98ada8eeei92ekf04teqemag9aabf2f4979caef6axajeof9akc49easb0amavc8fgfb54fifkfmb2d4c0fofqcbfsfufwesg0hgg2g8fyg4g6fdb9gcikgac2gfgggjexiigkaygoc7gmhkgqhnb4gscciogvgwcghjhrh0bcj4gyceh2h7hwh4hcb7bfhoh8jcigiwbbhehbiyj6hzciiqimezj0j2j8ckisjeiujahsi3cnbgbljghvjii8cojkcsjmibcrbojqbijocuk0jsi1bnjuk2ifi4cwi6brk4d0k6bscyjwbvksd3jzkxicfekkk8kukmkokqkyl1l8l2l4l6kblakelckclelgkhlikilk",
       "lead": {"Eb": 4.5, "Eq": 4, "Er": -2, "Zr": 1, "Zq": 2.5, "Yb": 2, "Zb": 1}, "gather": 1.3, "scatter": 3.2, "hop": 0.15, "pe": 0.42,
       "inp": 7.5, "lean": 0.8, "early": 1.5, "passes": 1, "fix": 0.06}
CFG["order"] = "000c0o020e0406080a0g0i24260s280q0k2a3g2s102e2q2k2w3q2m3i2h2j2o3n3a2d3c3l2v2y3t3p383e3v3w303632343z401243440m0u47480w0y1416181a1c1e1g1i1k1m1o1q1s1u1w1y20224b4c4h594l564i5b5e4u5g5j5l5s5c5o5w4q4n5y4y745v5n70614s7773629g4w68648c9i787b9o676b7c6d6f50888e9k7e8a7g6g7j8h6k7k6n6i7o9s8j7m8k7s8o7q6o6s8n528s7u5q6rao9u8r7x6w6u7y8w6y9mbwa18084daaq82a4d887d69ra7d4dm8z8udodedqdge2e4dudwdsdie6dk9w4fdye0dce89yadeaee9590eca2egag4peia8as92abbyaj96euaff098ek9ceqemax9a9eepakf2c4f4aub0anfgfic0f7fkc2f9fbfmc8fob2fqescafs54hgfufdfwfyg0g2c6gcgeg8b9gbccaycebcgjhkg6b4bfgoghexcghmgqhjikgkg4eycjhpjciwb7guckgmh0coiggshqh3hsgwcnblh7bbj4bogyhwiicqh4cuhzhchvh8ioi2hfhbi1imiyjebgi8j6j0j2bictjiibiqjgjaiubnj8jkd0isi4cwjmk0joi7d2jqjucziebrbsbuk2jwjsidfejzksk4klk6kukxkmkokqk8kyl1l2l8l4l6lalckbkclekelgkhkililk"
NB = 8
F32, BF, F16, I32, U16 = "float32", "bfloat16", "float16", "int32", "uint16"
SB = {"snd": (55, I32), "inp": (55, I32), "lu": (56, U16), "tb": (C, I32), "xi": (C, I32), "oi": (C, I32),
      "ic": (256, F32), "cd": (128, F32), "jc": (12, F32), "ri": (4, I32), "pc": (16, F32), "one": (128, BF), "cst": (32, BF),
      "id16": (16, BF), "w2": (144, BF), "wa": (144, BF), "blk": (128, BF), "indk": (8, BF), "idb": (128, BF), "keep0": (128, BF), "keep1": (128, BF),
      "ee": (256, BF), "kv": (768, BF), "tri": (128, F16), "dg": (128, F16), "mx": (144, F16), "zsrc": (2048, BF),
      "so": (12, U16), "so2": (2, U16), "vo": (240, BF), "vo2": (80, BF), "elu": (6, U16), "qm": (256, BF), "kl": (16, U16), "sf": (8, F32),
      "nxc": (656, I32), "nxq": (128, I32), "t16": (256, F16), "ql": (16, U16), "pb": (12 * 2048, BF),
      "rea": (272, BF), "ry": (288, BF), "zc": (656, BF), "zq": (128, BF), "zr": (136, BF), "zm": (128, BF), "rc": (800, BF), "rq": (128, BF),
      "rm": (768, BF), "q2": (256, BF), "r2": (384, BF), "mn": (16, F32), "md": (16, F32), "nw": (288, BF), "ms": (288, BF),
      "ll": (32, U16), "df": (272, BF), "sc": (4, F32), "sd": (32, F16), "ww": (288, BF), "fin": (29, F32), "finl": (29, F32),
      "rcl": (400, BF), "rcf": (384, F32), "ymf": (256, F32)}
STREAMS = ["b", "q", "r", "Eb", "Eq", "Yb", "Yq", "Zb", "Zq", "Er", "Zr"]
for _k in STREAMS:
    SB["g" + _k] = (2048, F16)
    SB["o" + _k] = (128, U16)
SCRATCH = {k: ("sbuf", [128, v[0]], v[1]) for k, v in SB.items()}
for _k in range(NB):
    SCRATCH["ps%d" % _k] = ("psum", [128, 512], F32)
SEMAPHORES = ["cV", "cA", "cP", "cG", "ld0", "ld1", "tb0", "tb1", "tb2", "tb3", "zf0", "zf1", "zf2", "oym", "oyr", "ofin", "oye",
              "linp", "lrc", "lfin", "ainp", "arc", "afin"]
R0 = 144


def v(buf, a=0, b=None, step=1, p=(0, 128)):
    return ("s", buf, a, SB[buf][0] if b is None else b, step, p)


def ps(tile, a, b, p=(0, 128)):
    return ("p", tile, a, b, 1, p)


def at(win, off):
    return ("i", win, off)


def col(j):
    return v("pc", j, j + 1)


def spans(x):
    if not isinstance(x, tuple):
        return []
    return spans(x[1]) + spans(x[2]) if x[0] == "i" else [x[:4]]


def size(x):
    return 16 * size(x[2]) if x[0] == "i" else (x[3] - x[2] + x[4] - 1) // x[4]


def make_ops(cfg):
    ops = []
    cyc = 0.00083

    def narrow(x):
        return x[0] == "s" and SB[x[1]][1] in (BF, F16, U16)

    def op(name, eng, calls, cost=None, r=(), w=(), sem=None, late=0.0):
        rd, wt = list(r), list(w)
        for m, a in calls:
            out = a[0][1] if a[0][0] == "i" else a[0]
            wt += spans(out)
            rd += [s for x in a[1:] for s in spans(x)] + (spans(a[0][2]) if a[0][0] == "i" else [])
        if cost is None:
            m, a = calls[0]
            if m == "matmul":
                cost = sum(max(min(64, size(a[1])), size(a[2])) for m, a in calls) * cfg["pe"] / 1000
            elif m == "iota":
                cost = 0.13 + 2 * cyc * size(a[0])
            elif a[0][0] == "i":
                cost = 0.05 + size(a[0]) * cfg["scatter"] / 1000
            elif isinstance(a[1], tuple) and a[1][0] == "i":
                cost = 0.06 + size(a[1]) * cfg["gather"] / 1000
            else:
                n = size(a[0] if m == "memset" else a[1])
                half = m in ("memset", "tensor_scalar", "lin") and narrow(a[0]) and (m == "memset" or narrow(a[1]))
                two = m == "tensor_tensor" and a[1][0] == a[2][0]
                cost = {e: cfg["fix"] + cyc * n * (0.5 if half and e == "V" else 2 if two else 1) for e in eng}
        ops.append({"n": name, "e": eng, "calls": calls, "c": cost if isinstance(cost, dict) else {e: cost for e in eng},
                    "r": rd, "w": wt, "sem": sem, "late": late})

    def lin(name, out, in_, scale=1.0, bias=0.0, eng="VA"):
        op(name, eng, [("lin", (out, in_, scale, bias))])

    def ts(name, out, in0, s1, s2, *o):
        op(name, "V", [("tensor_scalar", (out, in0, s1, s2) + o)])

    def tt(name, out, a, b, o):
        op(name, "V", [("tensor_tensor", (out, a, b, o))])

    def red(name, out, in_, o):
        op(name, "V", [("tensor_reduce", (out, in_, AxisListType.X, o))])

    def eq(buf, src, j):
        ts(buf, v(buf), v(src, 0, SB[buf][0]), col(j), None, AL.is_equal)

    def fill(name, x, val):
        op(name, "V", [("memset", (x, val))])

    def scat(name, win, off, src):
        op(name, "V", [("tensor_copy", (at(win, off), src))])

    def pe(name, seq, last=True):
        op(name, "P", [("matmul", (o, l, r, s, last and t)) for o, l, r, s, t in seq])

    def acc(out, terms):
        return [(out, l, r, i == 0, i == len(terms) - 1) for i, (l, r) in enumerate(terms)]

    def iota(x, pat, cm=0, base=0):
        op("i%s%d" % x[1:3], "G", [("iota", (x, pat, base, cm))])

    def hbm(name, idx):
        return ("d", name, 0, 1, idx)

    def dma(name, q, t, pairs, r=()):
        op(name, q, [("dma_start", x) for x in pairs], 0.06 * len(pairs), r=r, sem=name, late=t)

    def send(name, t0, t1, out, in_):
        op("l" + name, "G", [("remote_dma", (("x", name, 0, 1, out), in_))], 0.3, sem="l" + name, late=t0)
        op("a" + name, "X", [], 0.0, r=[("x", name, 0, 1)], w=spans(out), sem="a" + name, late=t1)

    ALL = slice(None)

    dma("ld0", "S", 1.6, [(v("snd", 0, 8), hbm("bk", ALL)), (v("snd", 8, 24), hbm("qs", ALL)), (v("snd", 24, 40), hbm("qc", ALL))])
    dma("ld1", "A", 1.6, [(v("snd", 40, 45), hbm("ex", ALL)), (v("snd", 45, 55), hbm("zs", ALL))])
    CH = cfg["chunks"]
    for k in range(len(CH) - 1):
        a, b = CH[k], CH[k + 1]
        dma("tb%d" % k, "S", 1.8 + 4.5 * b / C, [(v("tb", a, b), hbm("mt", (ALL, slice(a, b))))])
    iota(v("ri", 0, 1), [[0, 1]], 1)
    iota(v("ic"), [[1, 256]])
    iota(v("jc"), [[0, 3], [0, 2], [2048, 2]])
    iota(v("cd"), [[1, 8], [0, 16]])
    send("inp", cfg["inp"] - 3.5, 1.0, v("inp"), v("snd"))

    def pbv(k, n=1):
        return v("pb", 2048 * k, 2048 * (k + n))
    fill("zsrc", v("zsrc"), 0.0)
    fill("zp0", pbv(0), 0.0)
    lin("zp1", pbv(1), v("zsrc"), 0.0, 0.0, "A")
    for j in range(3):
        dma("zf%d" % j, "S", 3.5 + 3.3 * j, [(pbv(4 + 2 * j + i), v("zsrc")) for i in range(2)], r=[("x", "inp", 0, 1), ("s", "tb", 0, C)])

    def const(x, c):
        iota(x, [[0, size(x)]], base=c)

    const(pbv(2), 0)
    const(pbv(3), 0)
    iota(v("kv", 0, 256), [[0, 2], [1, 128]])
    const(v("one"), 1)
    iota(v("cst", 0, 8), [[-1, 8]])
    iota(v("cst", 8, 24), [[8, 2], [0, 8]], base=8)
    for x, c in ((v("cst", 24, 32), -8), (v("nw"), 0), (v("ms"), 0), (v("nxc", 128, 256), 0), (v("rea", 133, 144), 0), (v("ry", 133, 144), 0),
                 (v("ry", 272, 288), -1), (v("df", 129, 130), -64), (v("df", 265, 266), -64),
                 (v("rc", R0 + 128, R0 + 384), -1), (v("zc", 128, 384), -1)):
        const(x, c)
    iota(v("kv", 256, 768), [[0, 2], [1, 256]])
    const(pbv(10), 0)
    const(pbv(11), 0)

    for j, (c, o) in enumerate(((15, AL.bitwise_and), (4, AL.arith_shift_right), (16, AL.bitwise_and))):
        ts("ri%d" % (j + 1), v("ri", j + 1, j + 2), v("ri", 0, 1), c, None, o)
    lin("pc0", v("pc", 0, 4), v("ri"))
    for j, src, sc, bi in ((4, 1, -1.0, 527.0), (6, 2, 16.0, 15.0), (7, 3, 128.0, -2048.0), (8, 3, -128.0, 0.0), (9, 3, -64.0, 1024.0),
                           (10, 3, 64.0, 0.0), (13, 0, 1.0, -399.0)):
        lin("pc%d" % j, col(j), col(src), sc, bi)
    lin("pc5", col(5), col(1), 128.0, col(0))
    eq("id16", "ic", 1)
    lin("pc11", v("pc", 11, 13), v("id16", 0, 2), -1000.0, col(0))
    for buf, src, j in (("w2", "ic", 6), ("blk", "cd", 2), ("idb", "ic", 0), ("keep0", "ic", 11), ("keep1", "ic", 12)):
        eq(buf, src, j)
    ts("wa", v("wa"), v("ic", 0, 144), col(6), 1000.0, AL.not_equal, AL.mult)
    ts("indk", v("indk"), v("ic", 0, 8), col(2), -1024.0, AL.is_equal, AL.mult)
    ts("tri", v("tri"), v("ic", 0, 128), col(0), None, AL.is_gt)
    ts("dg", v("dg"), v("ic", 0, 128), col(0), col(13), AL.is_equal, AL.mult)
    tt("mx", v("mx", 0, 128), v("tri"), v("dg"), AL.add)
    lin("mx1", v("mx", 128, 144), v("zsrc", 0, 16), 0.0, 1.0)
    for h in range(2):
        lin("ee%d" % h, v("ee", 128 * h, 128 * h + 128), v("zsrc", 0, 128), 0.0, col(9 + h))
        lin("dfc%d" % h, v("df", 136 * h + 128, 136 * h + 129), col(1), -1.0 / 16, 0.0)
    lin("soc", v("so"), v("jc"), 1.0, col(5))
    lin("so2c", v("so2", 1, 2), col(5), 1.0, 2048.0)

    for k in range(len(CH) - 1):
        a, b = CH[k], CH[k + 1]
        lin("x%d" % k, v("xi", a, b), v("tb", a, b), 1.0 / 16, RND)
        ts("o%d" % k, v("oi", a, b), v("tb", a, b), 15, None, AL.bitwise_and)

    lin("lu", v("lu", 0, 55), v("inp"))
    lin("k0", v("kl", 0, 8), v("inp", 8, 16), 1.0 / 128, -0.5 + 1.0 / 256)
    lin("sf", v("sf"), v("inp", 16, 24), 2.0 ** -14, 0.0)
    lin("sod", v("so", 0, 12, 4), v("inp", 40, 55, 5), 128.0, col(0))
    lin("vo", v("vo"), at(v("id16"), v("lu", 40, 55)))
    for t in range(2):
        lin("qm%d" % t, v("qm", 128 * t, 128 * t + 128), at(v("id16"), v("lu", 24 + 8 * t, 32 + 8 * t)))
    for b, a, c in (("rea", 128, 40), ("ry", 128, 45), ("zr", 128, 50)):
        lin("let" + b, v(b, a, a + 5), v("inp", c, c + 5))

    def onehots(tag, w, vo, v0, so, s0):
        scat(tag + "a", pbv(4 * w, 2), v(so, s0, s0 + 2), v(vo, v0 + 16, v0 + 48))
        scat(tag + "b", pbv(4 * w + 2, 2), v("so", 2, 4), v(vo, v0 + 48, v0 + 80))

    for w in range(3):
        onehots("sp%d" % w, w, "vo", 80 * w, "so", 4 * w)

    def parts(s):
        n = cfg["cut"][s]
        return [(128 * i // n, 128 * (i + 1) // n) for i in range(n)]

    def gather(i, s, win, bias):
        for a, b in parts(s):
            lin("g%s%d_%d" % (s, i, a), v("g" + s, 16 * a, 16 * b), at(v(win), v("o" + s, a, b)), 1.0, bias)

    def pick(i, s, src, w, dst, d0, bias):
        base = 2048 * (4 * w + i - 1)
        for a, b in parts(s):
            tile = "%s%d_%d" % (s, i, a)
            pe("p" + tile, acc(ps(tile, 0, b - a), [(v("pb", base + 128 * j, base + 128 * j + 128), v("g" + src, 16 * a + j, 16 * b, 16))
                                                    for j in range(16)]))
            if i == 4 and s == "Zr":
                tt("dif1_%d" % a, v("df", 136 + a, 136 + b), ps(tile, 0, b - a), v("zm", a, b), AL.not_equal)
            lin("c" + tile, v(dst, d0 + a, d0 + b), ps(tile, 0, b - a), 1.0, bias)

    def walk(s, w, dst, d0, upto=5):
        pick(1, s, s[1], w, "o" + s, 0, HALF)
        for i in (2, 3):
            gather(i, s, "xi", -HALF)
            pick(i, s, s, w, "o" + s, 0, HALF)
        gather(4, s, "oi", 0.0)
        if upto > 4:
            pick(4, s, s, w, dst, d0, 0.0)

    def slide(tile, a, b, buf, c0, rhs, more=()):
        return acc(ps(tile, a, b), [(v(buf, c0 + 15 - r, c0 + 143 - r), rhs(r)) for r in range(16)] + list(more))

    def queries(t, s):
        a, ql = 128 * t, v("ql", 8 * t, 8 * t + 8)
        tt("qc%d" % t, v("t16", a, a + 128), at(v("nxc", 0, 128 + a), v("kl", 8 * t, 8 * t + 8)), v("qm", a, a + 128), AL.mult)
        pe("pq%d" % t, slide("q%d" % t, 0, 8, "w2", 0, lambda r: v("t16", a + r, a + 128, 16)))
        lin("cq%d" % t, ql, ps("q%d" % t, 0, 8), 1.0, HALF)
        lin("s0" + s, v("o" + s), at(v("xi"), ql))
        gather(1, s, "xi", -HALF)

    def row(a, b):
        return v("blk"), v("cst", a, b)

    def match(t, qb, rb, r0):
        a, kc, m0, n0 = 128 * t, 128 + 128 * t, 256 * t, 144 * t
        q, r = v(qb, 0, 128), v(rb, r0, r0 + kc)
        for h in range(2):
            lin("rm%d%d" % (t, h), v("rm", m0 + kc * h, m0 + kc * h + kc), r, col(7 + h), 0.0)
        op("r2%d" % t, "A", [("square", (v("r2", a, a + kc), r))])
        op("q2%d" % t, "A", [("square", (v("q2", a, a + 128), q))])
        for b in range(4):
            tile, p = "m%d%d" % (t, b), (32 * b, 32 * b + 32)
            pe("a" + tile, [(ps(tile, 0, 2 * kc), v("one", p=(p[0], p[0] + 1)), v("kv", m0, m0 + 2 * kc, p=(p[0], p[0] + 1)), True, True)]
               + [(ps(tile, kc * h, kc * h + kc), v("ee", 128 * h, 128 * h + 128, p=p), v("r2", a, a + kc, p=p), False, True) for h in range(2)],
               last=False)
            pe("b" + tile, [(ps(tile, 0, 2 * kc), v(qb, 0, 128, p=p), v("rm", m0, m0 + 2 * kc, p=p), False, True)])
            for h in range(2):
                j = 8 * t + 2 * b + h
                red("rd%d" % j, v("mn", j, j + 1), ps(tile, kc * h, kc * h + kc), AL.min)
        mn, md, new = v("mn", 8 * t, 8 * t + 8), v("md", 8 * t, 8 * t + 8), v("nw", n0 + 15, n0 + 143, 16)
        th, l, k, cu = ("%s%d" % (x, t) for x in ("th", "l", "hit", "cu"))
        pe("p" + th, acc(ps(th, 0, 8), [row(16, 24), (v("q2", a, a + 128), v("indk"))]))
        tt("new%d" % t, new, mn, ps(th, 0, 8), AL.is_ge)
        tt("md%d" % t, md, mn, ps(th, 0, 8), AL.subtract)
        n = 9 - t
        pe("p" + l, slide(l, 0, n, "nw", n0, lambda r: v("mx", r, 16 * n, 16), [row(0, n)]))
        lin("c" + l, v("ll", 16 * t, 16 * t + 8), ps(l, 0, 8), 1.0, col(4 + 10 * t))
        ts("ms%d" % t, v("ms", n0 + 15, n0 + 143, 16), md, 256.0, float(kc), AL.add, AL.min)
        pe("p" + k, slide(k, 0, 8, "ms", n0, lambda r: v("idb", r, 128, 16)))
        lin("c" + k, v("ll", 16 * t + 8, 16 * t + 16), ps(k, 0, 8))
        pe("p" + cu, acc(ps(cu, 0, 8), [row(24, 32), (v("tri"), new)] + [(v("one"), v("nw", 15, 143, 16))] * t))
        tt("ym%d" % t, v("rc", R0 + 384 + 8 * t, R0 + 392 + 8 * t), md, ps(cu, 0, 8), AL.min)

    def winner(t):
        d0, w0, sd, tile = 136 * t, 144 * t, v("sd", 16 * t, 16 * t + 16), "w%d" % t
        sc, gm = v("sc", 2 * t, 2 * t + 1), v("sc", 2 * t + 1, 2 * t + 2)
        red("sco%d" % t, sc, v("df", d0, d0 + 130), AL.add)
        lin("sd%d" % t, sd, v("id16"), sc, 0.0)
        pe("p" + tile, acc(ps(tile, 0, 16), [(v("blk"), sd)]))
        red("gm%d" % t, gm, ps(tile, 0, 16), AL.max)
        a, b = (15, 143) if t == 0 else (0, 144)
        ts("ww%d" % t, v("ww", w0 + a, w0 + b), v("wa", a, b), gm, sc, AL.add, AL.is_equal)

    lin("s0b", v("ob"), at(v("tb"), v("lu", 0, 8)), 1.0 / 16, RND)
    lin("nxb", v("nxc", 0, 128), at(v("tb"), v("lu", 0, 8)), 1.0 / 16, RND - HALF)
    gather(1, "b", "xi", -HALF)
    queries(0, "q")
    lin("nxq", v("nxq"), v("oq"), 1.0, -HALF)
    walk("Eb", 0, "rea", 144)
    walk("Eq", 0, "rea", 0)
    walk("Yb", 1, "ry", 144)
    walk("Yq", 1, "ry", 0)
    walk("Zb", 2, "zc", 0)
    walk("Zq", 2, "zq", 0)
    scat("clr", pbv(0), v("so", 0, 1), v("zsrc", 0, 16))
    match(0, "rea", "rea", 144)
    ts("k1", v("kl", 8, 16), v("sf"), ps("l0", 8, 9), -0.5 + 2.0 ** -15, AL.mult, AL.add)
    lin("pc14", col(14), ps("l0", 8, 9), 1.0, col(4))
    lin("pc14b", col(14), col(14), 1.0, -128.0)
    L0, L1 = v("ll", 0, 8), v("ll", 16, 24)
    scat("snx", v("nxc"), L0, v("nxq"))
    queries(1, "r")
    scat("szq", v("zc"), L0, v("zq"))
    tt("dif0", v("df", 0, 128), at(v("ry", 144, 288), v("ll", 8, 16)), v("ry", 0, 128), AL.not_equal)
    winner(0)
    pe("pu", acc(ps("u", 0, 272), [(v("keep0"), v("rea")), (v("ww", 15, 143), v("ry", 0, 272))]))
    lin("elu", v("elu", 0, 5), ps("u", 128, 133))
    lin("so2", v("so2", 0, 1), ps("u", 128, 129), 128.0, col(0))
    lin("urc", v("rc", 0, 272), ps("u", 0, 272))
    lin("vo2", v("vo2"), at(v("id16"), v("elu", 0, 5)))
    onehots("sq", 0, "vo2", 0, "so2", 0)
    scat("srt", v("rc", R0), L0, v("rc", 0, 128))

    walk("Er", 0, "rq", 0)
    walk("Zr", 2, "zr", 0, 4)
    match(1, "rq", "rc", R0)
    scat("srq", v("rc", R0), L1, v("rq"))
    send("rc", 2.0, 1.0, v("rcl"), v("rc", R0, R0 + 400))
    lin("rcf", v("rcf"), v("rcl", 0, 384))
    runs = [(max(16 * k - 14, 0), min(16 * k + 1, 128)) for k in range(9)]
    dma("oyr", "S", 2.0, [(("d", "yr", 0, 1, (slice(a, b), ALL)), v("rcf", p=(a, b))) for a, b in runs])
    pe("py", [(ps("y", 128 * t, 128 * t + 128, (0, 8)), v("rcl", 384 + 8 * t, 392 + 8 * t), v("idb"), True, True) for t in range(2)])
    lin("ymf", v("ymf", p=(0, 8)), ps("y", 0, 256, (0, 8)), 1.0, 256.0)
    dma("oym", "A", 1.6, [(hbm("ym", ALL), v("ymf", p=(0, 8)))])
    lin("zm", v("zm"), at(v("zc", 0, 272), v("ll", 24, 32)))
    pick(4, "Zr", "Zr", 2, "zr", 0, 0.0)
    winner(1)
    scat("szr", v("zc"), L1, v("zr", 0, 128))
    pe("pf", slide("f", 0, 24, "ww", 144, lambda r: v("zc", 24 * r, 24 * r + 24))
       + acc(ps("f", 24, 29), [(v("keep1"), v("rc", 128, 133)), (v("ww", 158, 286), v("zr", 128, 133))]))
    lin("fin", v("fin"), ps("f", 0, 29))
    send("fin", 1.0, 1.0, v("finl"), v("fin"))
    dma("ofin", "S", 1.6, [(("d", "yr", 1, 2, (slice(1, None, 16), ALL)), v("finl", 0, 24))])
    dma("oye", "A", 1.6, [(hbm("ye", ALL), v("finl", 24, 29))])
    return ops


def data_deps(ops):
    by, deps = {}, {}
    for o in ops:
        acc = [("r",) + x for x in o["r"]] + [("w",) + x for x in o["w"]]
        deps[o["n"]] = set(n2 for kind, m, b, lo, hi in acc for k2, l2, h2, n2 in by.get((m, b), [])
                           if "w" in (kind, k2) and (m == "p" or (lo < h2 and l2 < hi)))
        for kind, m, b, lo, hi in acc:
            by.setdefault((m, b), []).append((kind, lo, hi, o["n"]))
        o["pw"] = ([b for m, b, lo, hi in o["w"] if m == "p"] + [None])[0]
        o["pr"] = ([b for m, b, lo, hi in o["r"] if m == "p"] + [None])[0]
    return deps


def emit(g, T, peer, ops, deps, order):
    Q = {"V": g.vector, "A": g.scalar, "P": g.tensor, "G": g, "S": g.sync}
    rid, pid, mask, nen = peer
    left = {}
    for o in ops:
        left[o["pr"]] = left.get(o["pr"], 0) + 1
    free, bank_of, users = list(range(NB)), {}, {}
    chan, seq, know, done, plan, needed = {}, {}, {k: {} for k in Q}, {}, [], set()
    for o, e in order:
        n, d = o["n"], set(deps[o["n"]])
        if o["pw"]:
            d = set(x for x in d if chan[x][0] != "cP")
            if o["pw"] not in bank_of:
                b = bank_of[o["pw"]] = free.pop(0)
                d |= set(users.get(b, []))
                users[b] = []
        if o["pr"]:
            b = bank_of[o["pr"]]
            d |= set(u for u in users[b] if chan[u][0] != "c" + e)
            users[b].append(n)
            left[o["pr"]] -= 1
            if left[o["pr"]] == 0:
                free.append(b)
        seq[e] = seq.get(e, 0) + 1
        chan[n] = (o["sem"], 1) if o["sem"] else ("c" + e, seq[e])
        waits, done[n] = [], {}
        if e != "X":
            k = know[e]
            for x in sorted(d, key=lambda x: (-chan[x][1], x)):
                if k.get(chan[x][0], 0) < chan[x][1]:
                    waits.append(x)
                    needed.add(x)
                    for c2, v2 in done[x].items():
                        k[c2] = max(k.get(c2, 0), v2)
            done[n] = dict(k)
        done[n][chan[n][0]] = chan[n][1]
        plan.append((o, e, waits))
    count, val, waited = {}, {}, set()
    for o, e, waits in plan:
        if o["sem"]:
            val[o["n"]] = nen if e in "GX" else 16 * len(o["calls"])
        elif o["n"] in needed:
            count[e] = val[o["n"]] = count.get(e, 0) + 1

    def ap(x):
        if not isinstance(x, tuple):
            return x
        if x[0] == "i":
            return ap(x[1]).indirect(ap(x[2]))
        if x[0] == "d":
            return T[x[1]][x[4]]
        if x[0] == "x":
            return ap(x[4])
        return T[x[1] if x[0] == "s" else "ps%d" % bank_of[x[1]]][x[5][0]:x[5][1], x[2]:x[3]:x[4]]

    def call(e, m, a, sem, small):
        V = g.vector
        if m == "lin" and e == "V":
            return V.tensor_scalar(a[0], a[1], a[2], a[3], AL.mult, AL.add)
        if m == "lin":
            return g.scalar.activation(a[0], a[1], AF.Copy if isinstance(a[3], float) else AF.Identity, bias=a[3], scale=a[2])
        if m == "square":
            return g.scalar.activation(a[0], a[1], AF.Square)
        if m == "iota":
            return g.iota(*a, allow_small_or_imprecise_dtypes=True) if small else g.iota(*a)
        if m == "remote_dma":
            return g.remote_dma(a[0], a[1], T.sem["a" + sem[1:]], T.sem[sem], pid, rid, mask)
        if m == "dma_start":
            return Q[e].dma_start(*a).then_inc(T.sem[sem], 16)
        if m == "matmul":
            return g.tensor.matmul(*a)
        return {"memset": V.memset, "tensor_copy": V.tensor_copy, "tensor_scalar": V.tensor_scalar, "tensor_tensor": V.tensor_tensor,
                "tensor_reduce": V.tensor_reduce}[m](*a)

    for o, e, waits in plan:
        for x in waits:
            Q[e].wait_ge(T.sem[chan[x][0]], val[x])
            waited.add(x)
        for m, a in o["calls"]:
            ins = call(e, m, [ap(x) for x in a], o["sem"], m == "iota" and SB[a[0][1]][1] != I32)
        if o["n"] in needed and not o["sem"]:
            ins.then_inc(T.sem["c" + e], 1)
    for o, e, waits in plan:
        if o["sem"] and o["n"] not in waited:
            Q["G" if e == "G" else "S"].wait_ge(T.sem[o["sem"]], val[o["n"]])


def rank_program(g, core, T, topo):
    rank = T.rank_of(core)
    if rank is None:
        return
    n = len(T.cores)
    other = T.cores[(rank + n // 2) % n]
    rid, pid = topo.addr(other, core)
    ops = make_ops(CFG)
    deps = data_deps(ops)
    emit(g, T, (rid, pid, topo.mask(core, other), len(topo.engines(core, other))), ops, deps, parse(ops) if CFG.get("order") else deal(ops, deps, CFG))


def parse(ops):
    t = CFG["order"]
    return [(ops[x // 2], ops[x // 2]["e"][x % 2]) for x in (int(t[i:i + 2], 36) for i in range(0, len(t), 2))]


def deal(ops, deps, cfg):
    hop, by = cfg["hop"], {o["n"]: o for o in ops}
    num = {o["n"]: i for i, o in enumerate(ops)}
    succ = {o["n"]: [] for o in ops}
    for n, d in deps.items():
        for x in d:
            succ[x].append(n)
    jobs = {}
    for o in ops:
        jobs.setdefault(o["pw"] or o["pr"] or o["n"], []).append(o["n"])
    job = {n: j for j, m in jobs.items() for n in m}
    need = {j: set(job[x] for n in m for x in deps[n]) - {j} for j, m in jobs.items()}
    for e in "GS":
        line = [o["n"] for o in ops if o["e"] == e]
        for a, b in zip(line, line[1:]):
            need[b].add(a)
    lets = {j: [k for k in jobs if j in need[k]] for j in jobs}

    def lag(x, y):
        return by[x]["late"] + (0.0 if by[x]["e"] == by[y]["e"] == "P" else hop)

    def gap(line, t, c):
        for a, b in line:
            if t + c <= a + 1e-9:
                break
            t = max(t, b)
        return t

    way = {}
    for o in reversed(ops):
        way[o["n"]] = min([-o["late"]] + [way[x] - lag(o["n"], x) for x in succ[o["n"]]]) - min(o["c"].values())
    urge = {n: w - sum(x for k, x in cfg["lead"].items() if k in n) for n, w in way.items()}
    busy, when, life = {e: [] for e in "VAPGSX"}, {}, []
    left = {j: len(d) for j, d in need.items()}
    free = [j for j in jobs if not left[j]]

    def place(m, t0):
        prev = None
        for n in m:
            o, opts = by[n], []
            t = max([t0] + [when[y][1] + lag(y, n) for y in deps[n]] + [b for a, b in busy[o["e"][0]][-1:] if o["e"] in "GS"])
            for e in o["e"]:
                s = gap(busy[e], max(t, when[prev][1] + hop) if o["pr"] and when[prev][2] != e else t, o["c"][e])
                opts.append((s + o["c"][e] + cfg["lean"] * ((e == "A") == (o["c"][e] < 0.5)), s, e))
            f, s, e = min(opts)
            busy[e].append((s, s + o["c"][e]))
            busy[e].sort()
            when[n], prev = (s, s + o["c"][e], e), n

    while free:
        j = min(free, key=lambda k: (min(urge[n] for n in jobs[k]), num[jobs[k][0]]))
        free.remove(j)
        m, t0 = jobs[j], 0.0
        if by[m[0]]["pw"] and by[m[1]]["pw"]:
            t0 = max(when[y][1] for y in deps[m[1]] if y not in m) - cfg["early"]
        place(m, t0)
        while by[m[0]]["pw"]:
            a, b = when[m[0]][0], max(when[n][1] for n in m) + hop
            over = [(x, y) for x, y in life if x < b and a < y]
            if all(sum(1 for x, y in over if x <= p < y) < NB for p in [a] + [x for x, y in over if x > a]):
                life.append((a, b))
                break
            for n in m:
                busy[when[n][2]].remove(when[n][:2])
            place(m, min(y for x, y in over if y > a))
        for k in lets[j]:
            left[k] -= 1
            if not left[k]:
                free.append(k)
    return [(by[n], when[n][2]) for n in sorted(when, key=lambda n: (when[n][0], num[n]))]
